import numpy as np, ml_dtypes
CORES = [1,5,17,21,33,37,49,53]
N = 8
import mx_ref
BF = ml_dtypes.bfloat16
def gentries(a):
    return np.ascontiguousarray(a.reshape(8, 16, -1).transpose(0, 2, 1)).reshape(8, -1)
def gtable(e):
    e = np.asarray(e); return np.ascontiguousarray(e.reshape(8, -1, 16).transpose(0, 2, 1)).reshape(128, -1).astype(np.int32)
def gcols(t, e):
    v = np.concatenate([t.reshape(8, 16, -1, 4), np.zeros((8, 16, 1, 4), BF)], axis=2)
    return np.ascontiguousarray(np.stack([v[g][:, e[g]] for g in range(8)])).reshape(128, -1)
def gpick(z, e):
    return np.concatenate([z[16 * g:16 * g + 16][:, e[g]] for g in range(8)])
def tile(rs):
    return np.stack(rs, axis=2).reshape(128, -1).astype(BF)
def pick(q, e):
    c = np.concatenate([q[0].reshape(128, -1, 4), np.zeros((128, 1, 4), np.uint8)], axis=1); s = np.concatenate([q[1], np.ones((16, 1), np.uint8)], axis=1)
    return (np.ascontiguousarray(c[:, e].reshape(128, -1)), np.ascontiguousarray(s[:, e]))
def join(*qs):
    return (np.concatenate([q[0] for q in qs], axis=1), np.concatenate([q[1] for q in qs], axis=1))
def put(q, e, v):
    c, s = q[0].reshape(128, -1, 4).copy(), q[1].copy(); c[:, e] = v[0].reshape(128, -1, 4); s[:, e] = v[1]
    return (c.reshape(128, -1), s)
def pk(c, s):
    return (np.ascontiguousarray(c), mx_ref.live(s))
def emit(q):
    return q[0], q[1]
def packed(v, rng):
    q = [mx_ref.quantize(np.ascontiguousarray(v[r])) for r in range(N)]
    return np.stack([a for a, b in q]), np.stack([mx_ref.plane(b, rng) for a, b in q])
def values_of_codes():
    e, c = np.zeros((128, 128, 4), np.float32), np.zeros((128, 2, 4), np.uint8)
    e[np.arange(128), np.arange(128), 0] = 1
    c[:127, :, 0] = np.arange(256).reshape(2, 128).T[:127]
    return mx_ref.matmul(mx_ref.quantize(e.reshape(128, 512).astype(BF)), (c.reshape(128, 8), np.full((16, 2), 127, np.uint8))).T.reshape(-1).astype(np.float64)
CODE_VALUE, SCALE_VALUE = values_of_codes(), 2.0 ** (np.arange(256) - 127.0)
def decode(q):
    return (CODE_VALUE[q[0]].reshape(16, 8, -1, 4) * SCALE_VALUE[q[1]][:, None, :, None] + 0.0).reshape(128, -1).astype(np.float32)
def f(rng, *shape):
    return mx_ref.flush((rng.standard_normal(shape, dtype=np.float32) * np.exp2(rng.integers(-2, 3, shape[:-1] + (1,)))).astype(BF))
def wide(rng, *shape, cols=0):
    v = rng.standard_normal(shape, dtype=np.float32) * np.exp2(rng.integers(-12, 13, shape)).astype(np.float32)
    if cols: v *= np.repeat(np.exp2(rng.integers(-cols, cols + 1, shape[:-2] + (1, shape[-1] // 4))) * (rng.random(shape[:-2] + (1, shape[-1] // 4)) > 0.0625), 4, axis=-1).astype(np.float32)
    return mx_ref.flush(v.astype(BF))
C, E, B, K, R = 256, 16, 4, 64, 3
STEP = [1, 2, 4]
LO, HI = 2, 4
def gaps(p):
    return np.argmin(p[::16].reshape(8, E, E) + np.float32(0.0), axis=2)
def starts(a, c):
    s, free = np.full(a.shape, -1), np.zeros(c.shape, int)
    for k in range(B):
        n = a[:, :, k]
        i = np.where((c >= free) & (c < free + n), c + 1, free)
        fits = i + n <= E
        s[:, :, k] = np.where(fits, i, -1)
        free = np.where(fits, i + n + 1, free)
    return s
def solve(a, c):
    left = starts(a, c)
    m = starts(a[:, :, ::-1], E - 1 - c)[:, :, ::-1]
    end = E - 1 - m
    first, last = np.maximum(left, end - a + 1), np.minimum(left + a - 1, end)
    sure = (left >= 0) & (m >= 0) & (first <= last)
    line = E * np.arange(E)[None, :, None]
    return np.where(sure, line + left, -1).reshape(8, K), np.where(sure, line + end, -1).reshape(8, K), np.where(sure, first, -1), np.where(sure, last, -1)
def fallen(first, last):
    cell = np.arange(E)
    inside = (cell >= first[:, :, :, None]) & (cell <= last[:, :, :, None])
    e = np.where(inside.any(axis=2), B * cell[None, :, None] + np.argmax(inside, axis=2), -1)
    return np.ascontiguousarray(e.transpose(0, 2, 1)).reshape(8, C)
def numbers_of(rng):
    return {"x": np.array(f(rng, N, 128, 4 * C)), "u": np.array(f(rng, N, 128, 512)), "v": np.array(f(rng, N, 128, 512))}
def weights(rng, still=[]):
    w = np.array(f(rng, N, 128, 2048)).reshape(N, 8, 16, 4, 8, 16, 4)
    for i in still:
        w[:, :, i] = 0
        w[:, :, :, :, :, i] = 0
    c, p = packed(w.reshape(N, 128, 2048), rng)
    return {"wc": c, "ws": p}
def lengths(rng):
    return rng.integers(LO, HI + 1, (N, 8, E, B))
def blocks(a):
    return {"bl": np.stack([gtable(a[r].reshape(8, K)) for r in range(N)])}
def signs(rng):
    return np.stack([rng.permutation(8) % 2 * 2.0 - 1.0 for r in range(N)])
def setup_inputs(rng):
    return {**numbers_of(rng), **weights(rng), **blocks(lengths(rng))}
def setup_inputs_ties(rng):
    d = numbers_of(rng)
    e = rng.permutation(N)
    x = d["x"].reshape(N, 8, 16, C, 4)
    for r in range(N):
        for g in range(8):
            k = np.zeros(C, int) if r == e[0] else rng.permutation(C) % 3
            a = x[r, g, :8, :3].copy()
            a[:, 2] = 0
            x[r, g, :8] = a[:, k]
    x[e[1]] = 0
    u = d["u"].reshape(N, 8, 16, 8, 16, 4)
    k = u.copy()
    u[:, :, :, :, 0] = 0
    for g in range(8): u[:, g, :8, g, 0] = k[:, g, :8, g, 0]
    return {"x": x.reshape(N, 128, 4 * C), "u": u.reshape(N, 128, 512), "v": d["v"], **weights(rng, range(8)), **blocks(lengths(rng))}
def setup_inputs_near(rng):
    d = numbers_of(rng)
    x = d["x"].astype(np.float32).reshape(N, 8, 16, C, 4)
    u = d["u"].reshape(N, 128, 128, 4)
    u[:, :, ::16] = 0
    x[:, :, 0] = 0
    o, c, far = rng.permutation(N) % 4, signs(rng), signs(rng)
    j = np.arange(E)
    for r in range(N):
        i = (j + rng.integers(0, E, (8, E, 1))) % E
        twos = rng.integers(0, 2, (8, E, 1)) > 0
        if o[r] == 3:
            i = i % (E // 2) * 2 + j // (E // 2)
            twos = twos | True
        s = (np.where(twos, (E - 1 - i) // 2, E - 1 - i) + rng.integers(1, 200, (8, E, 1))).reshape(8, C)
        i = i.reshape(8, C)
        size = 1.0 if o[r] < 2 else 2.0 ** -4
        g = ((s[:, :, None] >> np.arange(8)) & 1) * np.exp2(np.arange(8) - 23.0) * size
        x[r, :, 8:] = rng.integers(4, 8, (8, 8, C, 4)) * 2.0 ** -20 * size
        x[r, :, 8] = g[:, :, :4]
        x[r, :, 9] = g[:, :, 4:]
        if o[r] < 2: x[r, :, 0, :, 0] = np.where((i == 0) & (far[r][:, None] > 0), 2.0 ** 30, c[r][:, None])
        if o[r] == 3:
            x[r, :, 10] = 0
            x[r, :, 10, :, 0] = (9 - i % 2) * 2.0 ** -30
        k = 1.0 if o[r] == 0 else 2.0 ** -30
        for h in range(0, 128, 16):
            u[r, h, h, 0] = k
            u[r, h + 8:h + 10, h] = k
            if o[r] == 3: u[r, h + 10, h, 0] = k
    return {"x": x.reshape(N, 128, 4 * C).astype(BF), "u": u.reshape(N, 128, 512), "v": d["v"], **weights(rng, [0, 8, 9, 10, 11, 12, 13, 14, 15]), **blocks(lengths(rng))}
def setup_inputs_huge(rng):
    d = numbers_of(rng)
    c = np.stack([rng.permutation(C) % 2 * 2.0 - 1.0 for r in range(N)])
    c[rng.permutation(N) < N // 2] = 1
    x = 2.0 ** 30 * (0.55 + 0.15 * rng.random((N, 128, C, 4))) * c[:, None, :, None]
    u = d["u"].reshape(N, 128, 128, 4)
    a = 2.0 ** 30 * (1 - 0.25 * rng.random((N, 128, 8, 4))) * signs(rng)[:, None, :, None]
    u[:, :, ::16] = a.astype(np.float32).astype(BF)
    w = np.zeros((N, 128, 4, 128, 4), np.float32)
    i = np.arange(128)
    for b in range(4): w[:, i, b, i, b] = -1
    wc, ws = packed(w.reshape(N, 128, 2048).astype(BF), rng)
    return {"x": x.astype(np.float32).reshape(N, 128, 4 * C).astype(BF), "u": u.reshape(N, 128, 512), "v": d["v"], "wc": wc, "ws": ws, **blocks(lengths(rng))}
def setup_inputs_packs(rng):
    d = numbers_of(rng)
    x = d["x"].reshape(N, 8, 16, C, 4)
    u = d["u"].reshape(N, 128, 128, 4)
    a = lengths(rng)
    gap = np.where(rng.random((N, 8, E)) < 0.25, rng.integers(0, 2, (N, 8, E)) * (E - 1), rng.integers(0, E, (N, 8, E)))
    ends = np.sort(np.argsort(rng.random((N, 8, E, E - B)), axis=3)[:, :, :, :B - 1], axis=3) + 1
    full = np.diff(ends, axis=3, prepend=0, append=E - B + 1)
    between = np.take_along_axis(ends + np.arange(B - 1), rng.integers(0, B - 1, (N, 8, E, 1)), axis=3)[:, :, :, 0]
    e = rng.permutation(N)
    long = np.arange(E)
    long = long[long % 4 < 2]
    for r in range(N):
        h = rng.permutation(8)
        a[r, h[0]] = 1
        a[r, h[1]] = E
        a[r, h[2]] = 1
        a[r, h[2], ::2, 0] = E - 1
        a[r, h[2], 1::2, B - 1] = E - 1
        a[r, h[2], long] = E
        a[r, h[2], long, long % 2 * (B - 1)] = E - 1
        gap[r, h[2], long] = (long // 4 + rng.integers(2)) % 2 * (E - 1)
        a[r, h[3]] = E // 2
        a[r, h[4]] = rng.integers(1, E + 1, (E, B))
        a[r, h[5]] = full[r, h[5]]
        gap[r, h[5], ::2] = between[r, h[5], ::2]
        a[r, h[6]] = E // B
    a[e[0]] = E
    a[e[1]] = full[e[1]]
    gap[e[1]] = between[e[1]]
    z = rng.integers(0, 2, (N, 8, E, E))
    np.put_along_axis(z, gap[:, :, :, None], -1, axis=3)
    x[:, :, 0, :, 0] = z.reshape(N, 8, C).astype(np.float32).astype(BF)
    u[:, :, ::16] = 0
    for h in range(0, 128, 16): u[:, h, h, 0] = 1
    return {"x": x.reshape(N, 128, 4 * C), "u": u.reshape(N, 128, 512), "v": d["v"], **weights(rng, [0]), **blocks(a)}
def setup_inputs_spread(rng):
    d = setup_inputs(rng)
    d["x"] = wide(rng, N, 128, 4 * C, cols=6)
    return d
def check_inputs(d):
    b = []
    for k in ("x", "u", "v"):
        a = np.abs(d[k].astype(np.float32))
        if not (np.isfinite(a).all() and ((a == 0) | (a >= 2.0 ** -30) & (a <= 2.0 ** 30)).all()): b.append("a value of " + k)
    if ((d["wc"] & 0x7F) == 0x7F).any(): b.append("a code of wc that is no number")
    none, least, most = [emit(mx_ref.quantize(np.full((128, 16), k, np.float32).astype(BF)))[1][0, 0] for k in (0.0, 2.0 ** -30, 2.0 ** 30)]
    for r in range(N):
        s = mx_ref.live(d["ws"][r])
        if ((s != none) & ((s < least) | (s > most))).any(): b.append("a scale of ws")
    if ((d["bl"] < 1) | (d["bl"] > E)).any(): b.append("a length in bl")
    return b
def reference(x, u, v, wc, ws, bl):
    qu = [mx_ref.quantize(u[r]) for r in range(N)]
    lay = [pk(wc[r], ws[r]) for r in range(N)]
    size = [gentries(bl[r]).reshape(8, E, B).astype(int) for r in range(N)]
    now = [x[r] for r in range(N)]
    for t in range(R):
        own, sent, bound = [], [], []
        for r in range(N):
            q = mx_ref.quantize(now[r])
            a = decode(q).astype(BF)
            e, h, first, last = solve(size[r], gaps(mx_ref.matmul(qu[r], q)))
            z = ((gcols(a, e).astype(np.float32) + gcols(a, h).astype(np.float32)) * np.float32(0.5)).astype(BF)
            own.append(a)
            sent.append(mx_ref.quantize(z))
            bound.append((first, last))
        for r in range(N):
            p = r ^ STEP[t]
            e = fallen(bound[p][0], bound[p][1])
            made = []
            for b in range(4):
                h = mx_ref.matmul(pick(lay[r], np.arange(128 * b, 128 * b + 128)), sent[p]) * np.float32(0.03125)
                h = np.concatenate([h, np.zeros((128, 1), np.float32)], axis=1)
                made.append(own[r][:, b::4].astype(np.float32) + gpick(h, e))
            now[r] = tile(made)
    y, ob = np.zeros((N, 128, C), np.float32), np.zeros((N, 8, 2 * K), np.float32)
    oc, osc = np.zeros((N, 128, 4 * C), np.uint8), np.zeros((N, 16, C), np.uint8)
    for r in range(N):
        q = mx_ref.quantize(now[r])
        y[r] = mx_ref.matmul(mx_ref.quantize(v[r]), q)
        ob[r] = np.stack([bound[r][0], bound[r][1]], axis=3).reshape(8, 2 * K)
        oc[r], osc[r] = emit(q)
    return {"y": y, "ob": ob, "oc": oc, "osc": osc}

@@ -1,0 +1,362 @@
+from concourse.mybir import dt, AluOpType, ActivationFunctionType
+
+C, K, R = 256, 64, 3
+PL = 272
+X4, U8, F32, BF, I32, U16 = "float8_e4m3fn_x4", "uint8", "float32", "bfloat16", "int32", "uint16"
+LW = 128 + K * R
+
+
+def sb(n, d):
+    return ("sbuf", [128, n], d)
+
+
+SCRATCH = {
+    "xin": sb(1024, BF), "uin": sb(512, BF), "vin": sb(512, BF), "blrow": sb(128, I32),
+    "wq": sb(512, X4), "wp": sb(512, U8), "uq": sb(128, X4), "up": sb(128, U8), "uq2": sb(128, X4), "up2": sb(128, U8),
+    "vq": sb(128, X4), "vp": sb(128, U8), "eq": sb(512, X4), "ep": sb(512, U8),
+    "xq": sb(256, X4), "xp": sb(256, U8), "xn": sb(1024, BF),
+    "lq": sb(LW, X4), "lp": sb(LW, U8), "zt": sb(512, BF),
+    "ebuf": sb(528, BF), "ones": sb(128, BF),
+    "ppin": sb(96, F32), "pp": sb(96, F32), "io32": sb(40, F32), "off": sb(48, U16),
+    "ccin": sb(128, F32), "cch": sb(128, F32), "ccn": sb(32, F32), "lidx": sb(256, BF), "ttin": sb(128, F32),
+    "c1": sb(128, BF), "c2": sb(256, BF), "g16": sb(128, BF), "j8": sb(128, F32), "w8in": sb(128, F32), "w8": sb(128, BF),
+    "cols": sb(8, F32), "bt": sb(128, F32), "an": sb(128, F32), "thr": sb(96, F32),
+    "d0": sb(512, F32), "d1": sb(512, F32), "o3": sb(512, F32), "qp": sb(128, F32), "ff": sb(128, F32), "gg": sb(64, F32),
+    "fs": sb(128, F32), "fd": sb(512, F32), "tab": sb(512, F32),
+    "mm": sb(256, F32), "dd": sb(256, BF), "gs": sb(256, BF), "ne": sb(128, BF), "se": sb(128, F32), "sf": sb(128, F32),
+    "oeh": sb(8, U16), "t2": sb(4 * PL, BF), "tf": sb(512, BF), "nn": sb(256, BF),
+    "lc": sb(16, U16), "nf": sb(128, BF), "cs": sb(128, BF),
+    "ha": sb(264, F32), "hb": sb(264, F32), "g2": sb(512, F32), "ob1": sb(16, F32), "ob2": sb(16, F32), "ob3": sb(16, F32),
+    "ys": sb(256, F32), "ps": ("psum", [128, 4096], F32),
+}
+for _t in range(R):
+    if _t:
+        SCRATCH["zq%d" % _t] = sb(128, X4)
+        SCRATCH["zp%d" % _t] = sb(128, U8)
+    SCRATCH["bd%d" % _t] = sb(8, F32)
+    SCRATCH["lb%d" % _t] = sb(8, F32)
+SEMAPHORES = ["sv", "sa", "sp", "sg", "dbl", "du", "dx", "dw", "dv", "dout", "sent"] + \
+    ["az%d" % t for t in range(R)] + ["ac%d" % t for t in range(R)]
+
+A = AluOpType
+AF = ActivationFunctionType
+BIG = 1e29
+SC = 16384.0
+
+
+def rank_program(g, core, T, topo):
+    rank = T.rank_of(core)
+    if rank is None:
+        return
+    Q = {"v": g.vector, "a": g.scalar, "p": g.tensor, "g": g, "s": g.sync}
+    cnt = {"v": 0, "a": 0, "p": 0, "g": 0}
+    seen = {q: {} for q in Q}
+
+    def wait(q, *toks):
+        for s, n in toks:
+            if seen[q].get(s, 0) < n:
+                Q[q].wait_ge(T.sem[s], n)
+                seen[q][s] = n
+
+    def done(q, ins):
+        cnt[q] += 1
+        ins.then_inc(T.sem["s" + q], 1)
+        return ("s" + q, cnt[q])
+
+    V = g.vector
+
+    def ms(ap, c, *d):
+        wait("v", *d)
+        return done("v", V.memset(ap, c))
+
+    def cp(o, i, *d):
+        wait("v", *d)
+        return done("v", V.tensor_copy(o, i))
+
+    def tr(o, i, *d):
+        wait("v", *d)
+        return done("v", V.transpose(o, i))
+
+    def tt(o, a, b, op, *d):
+        wait("v", *d)
+        return done("v", V.tensor_tensor(o, a, b, op))
+
+    def ts(o, a, s1, op0, s2, op1, *d):
+        wait("v", *d)
+        if op1 is None:
+            return done("v", V.tensor_scalar(o, a, s1, None, op0))
+        return done("v", V.tensor_scalar(o, a, s1, s2, op0, op1))
+
+    def scan(o, a, b, ini, op0, op1, *d):
+        wait("v", *d)
+        return done("v", V.tensor_tensor_scan(o, a, b, ini, op0, op1))
+
+    def qz(o, s, i, *d):
+        wait("v", *d)
+        return done("v", V.quantize_mx(o, s, i))
+
+    def act(o, i, f, scale, bias, *d):
+        wait("a", *d)
+        if bias is None and scale is None:
+            return done("a", g.scalar.activation(o, i, f))
+        if bias is None:
+            return done("a", g.scalar.activation(o, i, f, scale=scale))
+        return done("a", g.scalar.activation(o, i, f, bias=bias, scale=scale))
+
+    def mm(o, w, ws, x, xs, *d):
+        wait("p", *d)
+        return done("p", g.tensor.matmul_mx(o, w, ws, x, xs, True, True))
+
+    def iota(o, pat, base):
+        return done("g", g.iota(o, pat, base, 0, allow_small_or_imprecise_dtypes=True))
+
+    dn = {}
+
+    def dma(q, s, o, i, *d):
+        wait(q, *d)
+        Q[q].dma_start(o, i).then_inc(T.sem[s], 16)
+        dn[s] = dn.get(s, 0) + 16
+        return (s, dn[s])
+
+    def bank(b, n, a=0):
+        return T.ps[:, 512 * b + a:512 * b + n]
+
+    def blk(buf, b, n=128):
+        return buf[:, n * b:n * b + n]
+
+    off = T.off
+    m_bl = ms(T.blrow[:], 0)
+    k_bl = dma("s", "dbl", T.blrow[0:128:32, :], T.bl[:], m_bl)
+    k_u = dma("s", "du", T.uin[:], T.u[:])
+    k_x = dma("s", "dx", T.xin[:], T.x[:])
+    dma("s", "dw", T.wq[:].bitcast(dt.uint8), T.wc[:], k_x)
+    k_w = dma("s", "dw", T.wp[:], T.ws[:])
+    k_v = dma("s", "dv", T.vin[:], T.v[:])
+
+    m_one = ms(T.ones[:], 1.0)
+    m_e = ms(T.ebuf[:], 0.0)
+    iota(T.ppin[:, 0:32], [[0, 2], [4, 16]], 0)
+    i_pp = iota(T.ppin[:, 32:64], [[0, 2], [1, 4], [16, 4]], 0)
+    wait("g", m_e)
+    i_e = done("g", g.affine_select(T.ebuf[:, 3:515:4], T.ones[:], [[-1, 128]], A.is_equal, 0.0, 0, 1))
+    i_bl = iota(T.io32[:, 16:24], [[4, 4], [64, 2]], 0)
+    i_cc = iota(T.ccin[:], [[0, 4], [1, 32]], 0)
+    iota(T.io32[:, 8:16:2], [[32, 4]], 0)
+    iota(T.io32[:, 9:16:2], [[-32, 4]], 96)
+    i_ln = iota(T.io32[:, 0:8], [[16, 8]], 0)
+    i_lx = iota(T.lidx[:], [[4, 16], [0, 16]], 0)
+    iota(T.io32[:, 24:28], [[-128, 4]], 386)
+    iota(T.io32[:, 28:36], [[1, 2], [128, 4]], 66)
+    i_li = iota(T.io32[:, 36:40], [[-128, 4]], 387)
+    i_tt = iota(T.ttin[:], [[0, 8], [1, 16]], 0)
+    i_p2 = iota(T.ppin[:, 64:96], [[0, 4], [-1, 4], [4, 2]], 3)
+    i_j8 = iota(T.j8[:], [[1, 16], [0, 4], [-1, 2]], -64)
+    i_w8 = iota(T.w8in[:], [[0, 16], [-32, 4], [0, 2]], 96)
+
+    act(T.d1[:, 1:256:2], T.ones[:], AF.Copy, -100.0, None, m_one)
+    act(T.d1[:, 257:512:2], T.ones[:], AF.Copy, -100.0, None)
+    act(T.d0[:, 0:512:4], T.ones[:], AF.Copy, -100.0, None)
+    act(T.d0[:, 2:512:4], T.ones[:], AF.Copy, 8.0, None)
+    m_c1 = ms(T.c1[:], 0.0)
+    ms(T.d1[:, 2:128:4], 0.0)
+    ms(T.fs[:, 0:128:2], 0.0)
+    ms(T.zt[:, 256:512], 0.0)
+    ms(T.t2[:, 0:4 * PL:PL], 0.0)
+    ms(T.dd[:, 127:256:128], 0.0)
+    ms(T.c1[:, 0:128:16], BIG, m_c1)
+    v_pp = tr(T.pp[:, 0:64], T.ppin[:, 0:64], i_pp)
+    i4 = T.pp[:, 0:1]
+    v_e = [qz(blk(T.eq, b), blk(T.ep, b), T.ebuf[:, 3 - b:515 - b], i_e) for b in range(4)]
+    v_lb = ts(off[:, 16:24], T.io32[:, 16:24], T.pp[:, 32:33], A.add, None, None, v_pp, i_bl)
+
+    act(T.cols[:, 0:1], i4, AF.Identity, 4.0 / SC, 1.0 / SC, v_pp)
+    act(T.cols[:, 1:2], i4, AF.Identity, 4.0 / SC, 16.0 / SC)
+    a_cols = act(T.cols[:, 2:3], i4, AF.Identity, 0.5, 1.0)
+    a_cc = act(T.cch[:], T.ccin[:], AF.Abs, 1.0 / 64, -15.5 / 64, i_cc)
+    a_cn = act(T.ccn[:], T.cch[:, 0:32], AF.Copy, -1.0, None, a_cc)
+    a_d0 = act(T.d0[:, 1:512:4], T.cch[:], AF.Identity, 1.0, 0.5 / 64 - 9.0)
+
+    v_bt = ts(T.bt[:], T.blrow[:].indirect(off[:, 16:24]), -1.0 / 64, A.mult, None, None, k_bl, v_lb)
+    v_ln = cp(off[:, 0:16], T.io32[:, 0:16], i_ln)
+    v_an = tr(T.an[:], T.bt[:], v_bt)
+    a_n0 = act(T.d0[:, 3:128:4], T.an[:].indirect(off[:, 8:10]), AF.Identity, -1.0, 1.0 / 64, v_an, v_ln)
+    a_np = act(T.d0[:, 131:512:4], T.an[:].indirect(off[:, 10:16]), AF.Identity, -1.0, 1.0 / 64)
+
+    def sl(buf, s, a, step):
+        return buf[:, 128 * s + a:128 * s + 128:step]
+
+    def thr(s):
+        return [act(blk(T.thr, 2 * s - 2 + h, 16), blk(T.cch, h, 16), AF.Identity, 1.0, T.an[:, a:a + 1])
+                for h, a in enumerate((32 * s, 96 - 32 * s))][1]
+
+    def st_u(s, *d):
+        return tt(sl(T.d1, s, 0, 4), sl(T.d1, s, 2, 4), T.thr[:, 32 * s - 32:32 * s], A.is_gt, *d)
+
+    def st_place(s, *d):
+        return scan(sl(T.o3, s, 0, 1), sl(T.d0, s, 0, 1), sl(T.d1, s, 0, 1), 0.0, A.add, A.max, *d)
+
+    def st_fit(s, *d):
+        return ts(sl(T.d1, s, 0, 4), sl(T.o3, s, 3, 4), 17.0 / 64, A.is_gt, -1.0, A.mult, *d)
+
+    def st_free(s, *d):
+        return scan(sl(T.d1, s + 1, 0, 2), sl(T.o3, s, 1, 2), sl(T.d1, s, 0, 2), 0.0, A.add, A.max, *d)
+
+    def st_bad(s, *d):
+        return tt(sl(T.o3, s, 2, 4), sl(T.o3, s, 2, 4), sl(T.d1, s, 0, 4), A.subtract, *d)
+
+    def products(qx, *d):
+        s = [mm(bank(7 * h, 128), T.uq2[:], T.up2[:], blk(T.xq, h), blk(T.xp, h), qx[h], *d) for h in range(2)]
+        return s, [mm(bank(1 + b, C), blk(T.eq, b), blk(T.ep, b), T.xq[:], T.xp[:], v_e[b]) for b in range(4)]
+
+    def half_t(b, d):
+        return act(T.t2[:, PL * b + 1:PL * b + 257], bank(1 + b, C), AF.Copy, 0.5, None, d[b])
+
+    def gap_min(s):
+        return [scan(blk(T.mm, h), T.c1[:], bank(7 * h, 128), 0.0, A.add, A.min, s[h]) for h in range(2)]
+
+    def gap_less(m):
+        return [tt(T.dd[:, 128 * h:128 * h + 127], bank(7 * h, 128, 1), T.mm[:, 128 * h:128 * h + 127], A.is_lt, m[h])
+                for h in range(2)][1]
+
+    def gap_last(*d):
+        return scan(T.gs[:], T.c2[:], T.dd[:], 1.0, A.add, A.max, *d)
+
+    gp = T.gs[:, 255:256]
+
+    def gap_mask(*d):
+        return ts(T.ne[:], T.g16[:], gp, A.not_equal, None, None, *d)
+
+    x = tt(sl(T.d1, 0, 0, 4), T.an[:].indirect(off[:, 8:10]), T.ccn[:], A.is_lt, v_an, a_cn)
+    v_qu = qz(T.uq[:], T.up[:], T.uin[:], k_u)
+    x = st_place(0, x, a_d0, a_n0)
+    a_th = [None, thr(1)]
+    x = st_fit(0, x)
+    a_pu = act(T.up2[:], T.up[:].indirect(off[:, 0:8]), AF.Copy, None, None, v_qu)
+    a_th += [thr(2), thr(3)]
+    y = st_free(0, x)
+    st_bad(0)
+    x = st_u(1, y, a_th[1])
+    v_pu = cp(T.uq2[:].bitcast(dt.uint32), T.uq[:].bitcast(dt.uint32).indirect(off[:, 0:8]), v_qu)
+    x = st_place(1, x, a_np)
+    c2 = ts(T.c2[:], T.lidx[:], i4, A.is_equal, -1.0 / 32, A.mult, i_lx)
+    x = st_fit(1, x)
+    ts(T.c2[:, 15:256:16], T.lidx[:, 0:256:16], i4, A.is_equal, None, None, c2)
+    y = st_free(1, x)
+    st_bad(1)
+    x = st_u(2, y, a_th[2])
+    v_qx = [qz(blk(T.xq, 0), blk(T.xp, 0), blk(T.xin, 0, 512), k_x)]
+    x = st_place(2, x)
+    v_qx.append(qz(blk(T.xq, 1), blk(T.xp, 1), blk(T.xin, 1, 512)))
+    p_s, p_d = products(v_qx, v_pu, a_pu)
+    act(T.fd[:, 1:256:2], T.ttin[:], AF.Identity, -1.0 / 32, 2.0, i_tt)
+    act(T.fd[:, 257:512:2], T.ttin[:], AF.Identity, -1.0 / 32, 2.0)
+    a_g16 = act(T.g16[:], T.ttin[:], AF.Identity, -1.0 / 32, 2.0)
+    a_t2 = [half_t(b, p_d) for b in range(2)]
+    x = st_fit(2, x)
+    v_li = ts(off[:, 24:40], T.io32[:, 24:40], i4, A.add, None, None, i_li)
+    y = st_free(2, x)
+    st_bad(2)
+    x = st_u(3, y, a_th[3])
+    z = gap_min(p_s)
+    x = st_place(3, x)
+    a_qp = act(T.qp[:], T.o3[:].indirect(off[:, 32:40]), AF.Identity, -1.0, 17.0 / 64, x, v_li)
+    z = gap_less(z)
+    x = st_fit(3, x)
+    v_gp = gap_last(z)
+    x = st_bad(3, x, a_qp)
+    a_eh = act(T.fd[:, 128:256:2], T.o3[:].indirect(off[:, 28:32]), AF.Identity, -1.0 / 256, T.cols[:, 1:2], x)
+    a_ee = act(T.fd[:, 0:128:2], T.o3[:].indirect(off[:, 24:28]), AF.Identity, 1.0 / 256, T.cols[:, 0:1])
+    a_t2 += [half_t(2, p_d)]
+    v_ne = gap_mask(v_gp, a_g16)
+    v_p2 = tr(T.pp[:, 64:96], T.ppin[:, 64:96], i_p2)
+    v_ff = tt(T.ff[:], T.o3[:].indirect(off[:, 24:32]), T.qp[:], A.max, x)
+    cp(off[:, 40:48], T.pp[:, 64:72], v_p2)
+    act(T.fd[:, 256:384:2], T.ff[:, 0:64], AF.Identity, 1.0 / 256, -64.0 / SC, v_ff)
+    a_fl = act(T.fd[:, 384:512:2], T.ff[:, 64:128], AF.Identity, -1.0 / 256, -49.0 / SC)
+    a_t2 += [half_t(3, p_d)]
+    x = tt(T.gg[:], T.ff[:, 0:64], T.ff[:, 64:128], A.add, v_ff)
+    cp(T.w8[:, 1:128:2], T.w8in[:, 1:128:2], i_w8)
+    x = ts(T.fs[:, 1:128:2], T.gg[:], 15.0 / 64, A.is_le, None, None, x)
+    ts(T.w8[:, 0:128:2], T.w8in[:, 0:128:2], T.cols[:, 2:3], A.add, None, None, a_cols)
+    v_tab = scan(blk(T.tab, 1), T.fs[:], blk(T.fd, 1), 0.0, A.mult, A.add, x, a_eh)
+    v_tae = scan(blk(T.tab, 0), T.fs[:], blk(T.fd, 0), 0.0, A.mult, A.add, a_ee)
+    scan(blk(T.tab, 2), T.fs[:], blk(T.fd, 2), 0.0, A.mult, A.add, a_fl)
+    v_taf = scan(blk(T.tab, 3), T.fs[:], blk(T.fd, 3), 0.0, A.mult, A.add)
+
+    sent = [0]
+    v_qv = None
+    for t in range(R):
+        peer = T.cores[rank ^ (1 << t)]
+        rid, pid, _se = topo.addr(peer)
+        eng = topo.engines(core, peer)
+        mask = sum(1 << e for e in eng)
+        lo = 128 + K * t
+        if t > 0:
+            p_s, p_d = products(v_qx)
+            a_t2 = [half_t(b, p_d) for b in range(4)]
+            v_gp = gap_last(gap_less(gap_min(p_s)))
+            v_ne = gap_mask(v_gp)
+            v_tab = v_ne
+        x = scan(T.se[:, K:2 * K], T.ne[:, 0:K], T.tab[:, 129:256:2], 4.0, A.mult, A.max, v_ne, v_tab)
+        y = scan(T.se[:, 0:K], T.ne[:, 0:K], T.tab[:, 1:128:2], 4.0, A.mult, A.max, v_tae)
+        v_off = ts(T.oeh[:, 4:8], T.se[:, K + 15:2 * K:16], gp, A.subtract, SC, A.mult, x)
+        v_ofe = ts(T.oeh[:, 0:4], T.se[:, 15:K:16], gp, A.subtract, SC, A.mult, y)
+
+        def win(b):
+            return T.t2[:, PL * b:PL * b + 257]
+
+        a_n = [None] + [act(blk(T.nn, b, K), win(b).indirect(T.oeh[:, 4:8]), AF.Copy, None, None, v_off, a_t2[b])
+                        for b in range(1, 4)]
+        v_sf = scan(T.sf[:], T.ne[:], T.tab[:, 257:512:2], 4.0, A.mult, A.max, v_taf)
+        a_n[0] = cp(T.nn[:, 0:K], win(0).indirect(T.oeh[:, 4:8]), v_off, a_t2[0])
+        bd, lb = T["bd%d" % t], T["lb%d" % t]
+        v_bd = ts(bd[:], T.sf[:, 15:128:16], gp, A.subtract, SC, A.mult, v_sf)
+        wait("g", v_bd)
+        g.remote_dma(lb[:], bd[:], T.sem["ac%d" % t], T.sem.sent, pid, rid, mask)
+        for b in (1, 0, 2, 3):
+            x = tt(T.zt[:, b:256:4], win(b).indirect(T.oeh[:, 0:4]), blk(T.nn, b, K), A.add, a_n[b], v_ofe)
+        zq, zp = (T["zq%d" % t], T["zp%d" % t]) if t else (T.lq, T.lp)
+        v_qz = qz(zq[:, 0:128], zp[:, 0:128], T.zt[:], x)
+        wait("g", v_qz)
+        g.remote_dma(T.lq[:, lo:lo + K].bitcast(dt.uint8), zq[:, 0:K].bitcast(dt.uint8), T.sem["az%d" % t], T.sem.sent, pid, rid, mask)
+        g.remote_dma(T.lp[:, lo:lo + K], zp[:, 0:K], T.sem["az%d" % t], T.sem.sent, pid, rid, mask)
+        sent[0] += 3 * len(eng)
+        a_tf = [act(blk(T.tf, b, C), bank(1 + b, C), AF.Copy, None, None) for b in range(2)]
+        if t == 0:
+            ms(T.ha[:, 0:258:2], 0.0)
+            v_hz = ms(T.hb[:, 0:258:2], 0.0)
+        if t == 1:
+            v_qv = qz(T.vq[:], T.vp[:], T.vin[:], k_v)
+        if t == R - 1:
+            x = ts(T.ob1[:], bd[:].indirect(off[:, 40:41]), 0.0, A.is_lt, 65.0, A.mult)
+            x = tt(T.ob2[:], bd[:].indirect(off[:, 40:41]), T.ob1[:], A.add, x)
+            x = ts(T.ob3[:], T.ob2[:], -1.0, A.add, None, None, x)
+            dma("s", "dout", T.ob[:], T.ob3[:, 0:8], x)
+        x = tt(T.nf[:], lb[:].indirect(off[:, 40:48]), T.j8[:], A.is_gt, ("ac%d" % t, len(eng)), i_j8)
+        x = scan(T.cs[:], T.nf[:], T.w8[:], 128.0, A.mult, A.max, x)
+        v_lc = cp(T.lc[:], T.cs[:, 7:128:8], x)
+        hk = (0, 7, 5, 6)
+        p_h = [mm(bank(hk[b], 128), blk(T.wq, b), blk(T.wp, b), T.lq[:, lo - K:lo + K], T.lp[:, lo - K:lo + K],
+                  k_w, v_qz, ("az%d" % t, 2 * len(eng))) for b in range(4)]
+        v_h = [ts(T.ha[:, 128 * b + 1:128 * b + 128:2], bank(hk[b], 128, K), 0.03125, A.mult, None, None, p_h[b]) for b in range(2)]
+        a_h = [act(T.hb[:, 128 * b + 1:128 * b + 128:2], bank(hk[2 + b], 128, K), AF.Copy, 0.03125, None, p_h[2 + b], v_hz)
+               for b in range(2)]
+        a_g = [act(blk(T.g2, b, C), T.hb[:, 128 * b:128 * b + 129].indirect(T.lc[:]), AF.Copy, None, None, a_h[b], v_lc)
+               for b in range(2)]
+        for b in range(2):
+            tt(T.xn[:, b:1024:4], T.ha[:, 128 * b:128 * b + 129].indirect(T.lc[:]), blk(T.tf, b, C), A.add,
+               v_h[b], v_lc, a_tf[b])
+        tt(T.xn[:, 2:1024:4], blk(T.g2, 0, C), bank(3, C), A.add, a_g[0])
+        x = [tt(T.xn[:, 512 * h + 3:512 * h + 512:4], blk(T.g2, 2 + h), bank(4, 128 * h + 128, 128 * h), A.add, a_g[1])
+             for h in range(2)]
+        v_qx = [qz(blk(T.xq, h), blk(T.xp, h), blk(T.xn, h, 512), x[h]) for h in range(2)]
+
+    p_y = [mm(bank(7 * h, 128), T.vq[:], T.vp[:], blk(T.xq, h), blk(T.xp, h), v_qv, v_qx[h]) for h in range(2)]
+    y = act(T.ys[:, 0:128], bank(0, 128), AF.Copy, None, None, p_y[0])
+    x = cp(T.ys[:, 128:256], bank(7, 128), p_y[1])
+    dma("s", "dout", T.oc[:], T.xq[:].bitcast(dt.uint8), v_qx[1])
+    for k in range(4):
+        dma("a", "dout", T.osc[4 * k:4 * k + 4, :], T.xp[32 * k:32 * k + 4, :], v_qx[1])
+    last = dma("s", "dout", T.y[:], T.ys[:], x, y)
+    wait("g", ("sent", sent[0]), ("sg", cnt["g"]), ("sp", cnt["p"]), ("sv", cnt["v"]), ("sa", cnt["a"]))
+    wait("s", last)

@@ -1,7 +1,9 @@
+from concourse.bass import DstId, RemoteDMATransfer
 from concourse.mybir import dt, AluOpType, ActivationFunctionType
 
 C, K, R = 256, 64, 3
-PL = 272
+Z0 = 16
+PL = Z0 + C
 X4, U8, F32, BF, I32, U16 = "float8_e4m3fn_x4", "uint8", "float32", "bfloat16", "int32", "uint16"
 LW = 128 + K * R
 
@@ -17,25 +19,24 @@ SCRATCH = {
     "xq": sb(256, X4), "xp": sb(256, U8), "xn": sb(1024, BF),
     "lq": sb(LW, X4), "lp": sb(LW, U8), "zt": sb(512, BF),
     "ebuf": sb(528, BF), "ones": sb(128, BF),
-    "ppin": sb(96, F32), "pp": sb(96, F32), "io32": sb(40, F32), "off": sb(48, U16),
-    "ccin": sb(128, F32), "cch": sb(128, F32), "ccn": sb(32, F32), "lidx": sb(256, BF), "ttin": sb(128, F32),
-    "c1": sb(128, BF), "c2": sb(256, BF), "g16": sb(128, BF), "j8": sb(128, F32), "w8in": sb(128, F32), "w8": sb(128, BF),
-    "cols": sb(8, F32), "bt": sb(128, F32), "an": sb(128, F32), "thr": sb(96, F32),
-    "d0": sb(512, F32), "d1": sb(512, F32), "o3": sb(512, F32), "qp": sb(128, F32), "ff": sb(128, F32), "gg": sb(64, F32),
-    "fs": sb(128, F32), "fd": sb(512, F32), "tab": sb(512, F32),
-    "mm": sb(256, F32), "dd": sb(256, BF), "gs": sb(256, BF), "ne": sb(128, BF), "se": sb(128, F32), "sf": sb(128, F32),
-    "oeh": sb(8, U16), "t2": sb(4 * PL, BF), "tf": sb(512, BF), "nn": sb(256, BF),
+    "ppin": sb(128, F32), "pp": sb(128, F32), "io32": sb(16, F32), "off": sb(32, U16),
+    "tl": sb(128, BF), "lidx": sb(256, BF), "k0": sb(128, BF), "kj": sb(96, BF),
+    "c1": sb(128, BF), "c2": sb(256, BF), "g16": sb(64, BF), "j8": sb(128, F32), "w8": sb(128, BF),
+    "cols": sb(8, F32), "bt": sb(128, BF), "an": sb(128, BF),
+    "d0": sb(512, BF), "st": sb(640, BF), "l0": sb(192, BF), "l1": sb(192, BF), "lim": sb(192, BF),
+    "ww": sb(64, BF), "sg": sb(64, BF), "pi": sb(64, BF), "fs": sb(192, BF), "fd": sb(384, F32), "tab": sb(384, F32),
+    "mm": sb(256, F32), "dd": sb(256, BF), "gs": sb(256, BF), "ne": sb(64, BF), "se": sb(128, F32),
+    "oe": sb(8 * R, U16), "lb": sb(8 * R, U16), "lm": sb(4 * R + 4, F32), "up1": sb(32, F32), "dn1": sb(32, F32),
+    "lf": sb(8, F32), "bb": sb(16, F32), "of": sb(8, F32), "ob1": sb(16, F32), "ob2": sb(8, F32),
+    "t2": sb(4 * PL, BF), "tf": sb(512, BF), "nn": sb(256, BF),
     "lc": sb(16, U16), "nf": sb(128, BF), "cs": sb(128, BF),
-    "ha": sb(264, F32), "hb": sb(264, F32), "g2": sb(512, F32), "ob1": sb(16, F32), "ob2": sb(16, F32), "ob3": sb(16, F32),
+    "ha": sb(264, F32), "hb": sb(264, F32), "g2": sb(640, F32),
     "ys": sb(256, F32), "ps": ("psum", [128, 4096], F32),
 }
-for _t in range(R):
-    if _t:
-        SCRATCH["zq%d" % _t] = sb(128, X4)
-        SCRATCH["zp%d" % _t] = sb(128, U8)
-    SCRATCH["bd%d" % _t] = sb(8, F32)
-    SCRATCH["lb%d" % _t] = sb(8, F32)
-SEMAPHORES = ["sv", "sa", "sp", "sg", "dbl", "du", "dx", "dw", "dv", "dout", "sent"] + \
+for _t in range(1, R):
+    SCRATCH["zq%d" % _t] = sb(128, X4)
+    SCRATCH["zp%d" % _t] = sb(128, U8)
+SEMAPHORES = ["sv", "sa", "sp", "sg", "dbl", "du", "dx", "dw", "dv", "dout", "sent", "am"] + \
     ["az%d" % t for t in range(R)] + ["ac%d" % t for t in range(R)]
 
 A = AluOpType
@@ -103,6 +104,12 @@ def rank_program(g, core, T, topo):
             return done("a", g.scalar.activation(o, i, f, scale=scale))
         return done("a", g.scalar.activation(o, i, f, bias=bias, scale=scale))
 
+    def lin(o, i, scale, bias, *d):
+        return act(o, i, AF.Identity, scale, bias, *d)
+
+    def fill(o, n, c, *d):
+        return act(o, T.ones[:, 0:n], AF.Copy, c, None, *d)
+
     def mm(o, w, ws, x, xs, *d):
         wait("p", *d)
         return done("p", g.tensor.matmul_mx(o, w, ws, x, xs, True, True))
@@ -124,239 +131,310 @@ def rank_program(g, core, T, topo):
     def blk(buf, b, n=128):
         return buf[:, n * b:n * b + n]
 
+    def bits(engines):
+        return sum(1 << e for e in engines)
+
     off = T.off
+    peers = [T.cores[rank ^ (1 << t)] for t in range(R)]
     m_bl = ms(T.blrow[:], 0)
     k_bl = dma("s", "dbl", T.blrow[0:128:32, :], T.bl[:], m_bl)
     k_u = dma("s", "du", T.uin[:], T.u[:])
     k_x = dma("s", "dx", T.xin[:], T.x[:])
-    dma("s", "dw", T.wq[:].bitcast(dt.uint8), T.wc[:], k_x)
+    dma("s", "dw", T.wq[:].bitcast(dt.uint8), T.wc[:], k_u)
     k_w = dma("s", "dw", T.wp[:], T.ws[:])
-    k_v = dma("s", "dv", T.vin[:], T.v[:])
 
     m_one = ms(T.ones[:], 1.0)
     m_e = ms(T.ebuf[:], 0.0)
-    iota(T.ppin[:, 0:32], [[0, 2], [4, 16]], 0)
-    i_pp = iota(T.ppin[:, 32:64], [[0, 2], [1, 4], [16, 4]], 0)
+    i_pp = iota(T.ppin[:, 0:32], [[0, 2], [1, 4], [16, 4]], 0)
+    i_bl = iota(T.io32[:, 0:8], [[4, 4], [64, 2]], 0)
     wait("g", m_e)
     i_e = done("g", g.affine_select(T.ebuf[:, 3:515:4], T.ones[:], [[-1, 128]], A.is_equal, 0.0, 0, 1))
-    i_bl = iota(T.io32[:, 16:24], [[4, 4], [64, 2]], 0)
-    i_cc = iota(T.ccin[:], [[0, 4], [1, 32]], 0)
-    iota(T.io32[:, 8:16:2], [[32, 4]], 0)
-    iota(T.io32[:, 9:16:2], [[-32, 4]], 96)
-    i_ln = iota(T.io32[:, 0:8], [[16, 8]], 0)
-    i_lx = iota(T.lidx[:], [[4, 16], [0, 16]], 0)
-    iota(T.io32[:, 24:28], [[-128, 4]], 386)
-    iota(T.io32[:, 28:36], [[1, 2], [128, 4]], 66)
-    i_li = iota(T.io32[:, 36:40], [[-128, 4]], 387)
-    i_tt = iota(T.ttin[:], [[0, 8], [1, 16]], 0)
-    i_p2 = iota(T.ppin[:, 64:96], [[0, 4], [-1, 4], [4, 2]], 3)
-    i_j8 = iota(T.j8[:], [[1, 16], [0, 4], [-1, 2]], -64)
-    i_w8 = iota(T.w8in[:], [[0, 16], [-32, 4], [0, 2]], 96)
+    i_tl = iota(T.tl[:], [[0, 4], [1, 16], [0, 2]], 0)
+    iota(T.ppin[:, 32:64], [[0, 16], [-2, 2]], 1)
+    i_lk = iota(T.io32[:, 8:16], [[32, 4], [0, 2]], -48)
+    iota(T.ppin[:, 64:96], [[0, 2], [1, 16]], 0)
+    i_p2 = iota(T.ppin[:, 96:128], [[0, 4], [-2, 4], [7, 2]], 7)
+    i_lx = iota(T.lidx[:], [[1, 16], [0, 16]], 0)
 
-    act(T.d1[:, 1:256:2], T.ones[:], AF.Copy, -100.0, None, m_one)
-    act(T.d1[:, 257:512:2], T.ones[:], AF.Copy, -100.0, None)
-    act(T.d0[:, 0:512:4], T.ones[:], AF.Copy, -100.0, None)
-    act(T.d0[:, 2:512:4], T.ones[:], AF.Copy, 8.0, None)
+    fill(T.d0[:, 0:512:4], 128, -100.0, m_one)
+    fill(T.st[:, 3:128:4], 32, 49.0 / 64)
+    fill(T.l0[:, 0:192:2], 96, 0.0)
+    fill(T.fs[:, 0:192:3], 64, 0.0)
+    fill(T.fd[:, 1:384:3], 128, 0.0)
+    for b in range(4):
+        fill(T.t2[:, PL * b:PL * b + Z0], Z0, 0.0)
     m_c1 = ms(T.c1[:], 0.0)
-    ms(T.d1[:, 2:128:4], 0.0)
-    ms(T.fs[:, 0:128:2], 0.0)
     ms(T.zt[:, 256:512], 0.0)
-    ms(T.t2[:, 0:4 * PL:PL], 0.0)
     ms(T.dd[:, 127:256:128], 0.0)
     ms(T.c1[:, 0:128:16], BIG, m_c1)
-    v_pp = tr(T.pp[:, 0:64], T.ppin[:, 0:64], i_pp)
-    i4 = T.pp[:, 0:1]
+    v_pp = tr(T.pp[:, 0:32], T.ppin[:, 0:32], i_pp)
+    v_lb = ts(off[:, 0:8], T.io32[:, 0:8], T.pp[:, 0:1], A.add, None, None, v_pp, i_bl)
     v_e = [qz(blk(T.eq, b), blk(T.ep, b), T.ebuf[:, 3 - b:515 - b], i_e) for b in range(4)]
-    v_lb = ts(off[:, 16:24], T.io32[:, 16:24], T.pp[:, 32:33], A.add, None, None, v_pp, i_bl)
 
-    act(T.cols[:, 0:1], i4, AF.Identity, 4.0 / SC, 1.0 / SC, v_pp)
-    act(T.cols[:, 1:2], i4, AF.Identity, 4.0 / SC, 16.0 / SC)
-    a_cols = act(T.cols[:, 2:3], i4, AF.Identity, 0.5, 1.0)
-    a_cc = act(T.cch[:], T.ccin[:], AF.Abs, 1.0 / 64, -15.5 / 64, i_cc)
-    a_cn = act(T.ccn[:], T.cch[:, 0:32], AF.Copy, -1.0, None, a_cc)
-    a_d0 = act(T.d0[:, 1:512:4], T.cch[:], AF.Identity, 1.0, 0.5 / 64 - 9.0)
+    t32 = T.tl[:, 0:32]
+    a_ab = act(blk(T.k0, 3, 32), t32, AF.Abs, 1.0 / 64, -7.5 / 64, i_tl)
+    lin(T.st[:, 2:128:4], t32, 1.0 / 64, 48.0 / 64)
+    lin(blk(T.k0, 0, 32), t32, 1.0 / 64, 48.0 / 64)
+    lin(blk(T.k0, 1, 32), t32, -1.0 / 64, -48.0 / 64)
+    lin(blk(T.k0, 2, 32), blk(T.k0, 3, 32), 1.0, -55.5 / 64, a_ab)
+    a_k0 = lin(T.kj[:], T.tl[:, 0:96], 1.0 / 64, -63.0 / 64)
+    lin(T.l1[:, 0:192:2], T.tl[:, 0:96], 1.0 / 64, 1.0 / 64)
 
-    v_bt = ts(T.bt[:], T.blrow[:].indirect(off[:, 16:24]), -1.0 / 64, A.mult, None, None, k_bl, v_lb)
-    v_ln = cp(off[:, 0:16], T.io32[:, 0:16], i_ln)
+    v_bt = ts(T.bt[:], T.blrow[:].indirect(off[:, 0:8]), 1.0 / 64, A.mult, -63.0 / 64, A.add, k_bl, v_lb)
+    x = tr(T.pp[:, 32:64], T.ppin[:, 32:64], i_lk)
     v_an = tr(T.an[:], T.bt[:], v_bt)
-    a_n0 = act(T.d0[:, 3:128:4], T.an[:].indirect(off[:, 8:10]), AF.Identity, -1.0, 1.0 / 64, v_an, v_ln)
-    a_np = act(T.d0[:, 131:512:4], T.an[:].indirect(off[:, 10:16]), AF.Identity, -1.0, 1.0 / 64)
+    v_lk = ts(off[:, 8:16], T.io32[:, 8:16], T.pp[:, 32:33], A.mult, 48.0, A.add, x)
+    v_lu = ts(off[:, 16:24], T.tl[:, 0:16:2], 16.0, A.mult, None, None)
+    a_mf = lin(blk(T.lm, R, 4), T.an[:, 0:128:32], 64.0, 62.0, v_an)
+    a_n = act(T.d0[:, 1:512:4], T.an[:].indirect(off[:, 8:16]), AF.Copy, None, None, v_lk)
+    a_n3 = lin(T.d0[:, 3:512:4], T.d0[:, 1:512:4], -1.0, -63.0 / 64, a_n)
+    a_th = act(T.l1[:, 1:192:2], T.d0[:, 129:512:4], AF.Copy, -1.0, None)
 
-    def sl(buf, s, a, step):
-        return buf[:, 128 * s + a:128 * s + 128:step]
+    allowed = [topo.engines(core, p) for p in peers]
+    narrow = min(allowed, key=len)
+    far = [t for t in range(R) if len(allowed[t]) == len(narrow)]
+    near = [t for t in range(R) if t not in far]
+    share = {}
+    for n, t in enumerate(far):
+        share[t] = narrow[n * len(narrow) // len(far):(n + 1) * len(narrow) // len(far)]
+    for t in near:
+        share[t] = [e for e in allowed[t] if e not in narrow]
+    wait("g", a_mf)
+    g.remote_dma_fused([RemoteDMATransfer(dst_ids=[DstId(rid=topo.addr(peers[t])[0], pnc=topo.addr(peers[t])[1])],
+                                          dma_engine_mask=bits(share[t]), remote_sem=T.sem.am,
+                                          src=blk(T.lm, R, 4), dst=blk(T.lm, t, 4)) for t in range(R)], local_sem=T.sem.sent)
+    sent = [sum(len(share[t]) for t in range(R))]
+    k_m = ("am", sent[0])
 
-    def thr(s):
-        return [act(blk(T.thr, 2 * s - 2 + h, 16), blk(T.cch, h, 16), AF.Identity, 1.0, T.an[:, a:a + 1])
-                for h, a in enumerate((32 * s, 96 - 32 * s))][1]
+    def sl(buf, s, a):
+        return buf[:, 128 * s + a:128 * s + 128:4]
 
-    def st_u(s, *d):
-        return tt(sl(T.d1, s, 0, 4), sl(T.d1, s, 2, 4), T.thr[:, 32 * s - 32:32 * s], A.is_gt, *d)
+    def lanes(buf, s):
+        return buf[:, 64 * s - 63:64 * s:2]
 
-    def st_place(s, *d):
-        return scan(sl(T.o3, s, 0, 1), sl(T.d0, s, 0, 1), sl(T.d1, s, 0, 1), 0.0, A.add, A.max, *d)
+    def tests(s, *d):
+        tt(sl(T.st, s, 0), sl(T.st, s, 2), lanes(T.l1, s), A.is_gt, *d)
+        tt(sl(T.st, s, 1), sl(T.st, s, 2), sl(T.d0, s, 1), A.add)
+        return tt(sl(T.d0, s, 2), sl(T.st, s, 2), lanes(T.lim, s), A.is_le, v_lim)
 
-    def st_fit(s, *d):
-        return ts(sl(T.d1, s, 0, 4), sl(T.o3, s, 3, 4), 17.0 / 64, A.is_gt, -1.0, A.mult, *d)
+    def place(s, *d):
+        return scan(blk(T.st, s + 1), blk(T.d0, s), blk(T.st, s), 0.0, A.add, A.max, *d)
 
-    def st_free(s, *d):
-        return scan(sl(T.d1, s + 1, 0, 2), sl(T.o3, s, 1, 2), sl(T.d1, s, 0, 2), 0.0, A.add, A.max, *d)
+    def left(buf, a):
+        return buf[:, a:a + 505:8]
 
-    def st_bad(s, *d):
-        return tt(sl(T.o3, s, 2, 4), sl(T.o3, s, 2, 4), sl(T.d1, s, 0, 4), A.subtract, *d)
+    def right(buf, a):
+        return buf[:, a + 508:a + 3:-8]
+
+    dbank = {(0, 0): 1, (0, 1): 5, (1, 0): 2, (1, 1): 6}
+
+    def score(h, *d):
+        return mm(bank(7 * h, 128), T.uq2[:], T.up2[:], blk(T.xq, h), blk(T.xp, h), *d)
 
     def products(qx, *d):
-        s = [mm(bank(7 * h, 128), T.uq2[:], T.up2[:], blk(T.xq, h), blk(T.xp, h), qx[h], *d) for h in range(2)]
-        return s, [mm(bank(1 + b, C), blk(T.eq, b), blk(T.ep, b), T.xq[:], T.xp[:], v_e[b]) for b in range(4)]
+        s, p = [], {}
+        for h in range(2):
+            s.append(score(h, qx[h], *d))
+            for b in range(2):
+                p[b, h] = mm(bank(dbank[b, h], 128), blk(T.eq, b), blk(T.ep, b), blk(T.xq, h), blk(T.xp, h), v_e[b])
+        for b in range(2, 4):
+            p[b] = mm(bank(1 + b, C), blk(T.eq, b), blk(T.ep, b), T.xq[:], T.xp[:], v_e[b])
+        return s, p
 
-    def half_t(b, d):
-        return act(T.t2[:, PL * b + 1:PL * b + 257], bank(1 + b, C), AF.Copy, 0.5, None, d[b])
+    def half_t(key, p):
+        if key in dbank:
+            a = PL * key[0] + Z0 + 128 * key[1]
+            return act(T.t2[:, a:a + 128], bank(dbank[key], 128), AF.Copy, 0.5, None, p[key])
+        return act(T.t2[:, PL * key + Z0:PL * key + PL], bank(1 + key, C), AF.Copy, 0.5, None, p[key])
 
-    def gap_min(s):
-        return [scan(blk(T.mm, h), T.c1[:], bank(7 * h, 128), 0.0, A.add, A.min, s[h]) for h in range(2)]
+    def gap_min(h, *d):
+        return scan(blk(T.mm, h), T.c1[:], bank(7 * h, 128), 0.0, A.add, A.min, *d)
 
-    def gap_less(m):
-        return [tt(T.dd[:, 128 * h:128 * h + 127], bank(7 * h, 128, 1), T.mm[:, 128 * h:128 * h + 127], A.is_lt, m[h])
-                for h in range(2)][1]
+    def gap_less(h, *d):
+        return tt(T.dd[:, 128 * h:128 * h + 127], bank(7 * h, 128, 1), T.mm[:, 128 * h:128 * h + 127], A.is_lt, *d)
 
-    def gap_last(*d):
-        return scan(T.gs[:], T.c2[:], T.dd[:], 1.0, A.add, A.max, *d)
+    def gap_last(h, *d):
+        return scan(blk(T.gs, h), blk(T.c2, h), blk(T.dd, h), T.gs[:, 127:128] if h else 1.0, A.add, A.max, *d)
 
     gp = T.gs[:, 255:256]
 
     def gap_mask(*d):
         return ts(T.ne[:], T.g16[:], gp, A.not_equal, None, None, *d)
 
-    x = tt(sl(T.d1, 0, 0, 4), T.an[:].indirect(off[:, 8:10]), T.ccn[:], A.is_lt, v_an, a_cn)
+    k_0 = T.an[:].indirect(off[:, 8:10])
+    tt(sl(T.st, 0, 0), k_0, blk(T.k0, 1, 32), A.is_gt, v_an, v_lk, a_k0)
+    tt(sl(T.st, 0, 1), k_0, blk(T.k0, 0, 32), A.add)
+    x = tt(sl(T.d0, 0, 2), k_0, blk(T.k0, 2, 32), A.is_le)
+    y = tt(T.l0[:, 1:192:2], T.an[:].indirect(off[:, 10:16]), T.kj[:], A.is_le)
+    x = place(0, x, a_n3)
+    v_lim = scan(T.lim[:], T.l0[:], T.l1[:], 0.0, A.mult, A.add, y, a_th)
+    x = tests(1, x)
     v_qu = qz(T.uq[:], T.up[:], T.uin[:], k_u)
-    x = st_place(0, x, a_d0, a_n0)
-    a_th = [None, thr(1)]
-    x = st_fit(0, x)
-    a_pu = act(T.up2[:], T.up[:].indirect(off[:, 0:8]), AF.Copy, None, None, v_qu)
-    a_th += [thr(2), thr(3)]
-    y = st_free(0, x)
-    st_bad(0)
-    x = st_u(1, y, a_th[1])
-    v_pu = cp(T.uq2[:].bitcast(dt.uint32), T.uq[:].bitcast(dt.uint32).indirect(off[:, 0:8]), v_qu)
-    x = st_place(1, x, a_np)
-    c2 = ts(T.c2[:], T.lidx[:], i4, A.is_equal, -1.0 / 32, A.mult, i_lx)
-    x = st_fit(1, x)
-    ts(T.c2[:, 15:256:16], T.lidx[:, 0:256:16], i4, A.is_equal, None, None, c2)
-    y = st_free(1, x)
-    st_bad(1)
-    x = st_u(2, y, a_th[2])
+    a_pu = act(T.up2[:], T.up[:].indirect(off[:, 16:24]), AF.Copy, None, None, v_qu, v_lu)
+    x = place(1, x)
+    v_p2 = tr(T.pp[:, 64:128], T.ppin[:, 64:128], i_p2)
+    line = T.pp[:, 64:65]
+    lin(T.cols[:, 0:1], line, 16.0 / SC, (Z0 - 64.0) / SC, v_p2)
+    lin(T.cols[:, 1:2], line, 16.0 / SC, (Z0 + 64.0) / SC)
+    lin(T.cols[:, 2:3], line, 2.0, 1.0)
+    a_cols = lin(T.cols[:, 3:4], line, 16.0, float(Z0))
+    for h in range(2):
+        lin(T.fd[:, 192 * h + 2:192 * h + 192:3], T.tl[:, 0:128:2], -1.0 / 32 - 1.0 / SC, 2.0 + 15.0 / SC)
+    a_g16 = lin(T.g16[:], T.tl[:, 0:128:2], -1.0 / 32, 2.0)
+    x = tests(2, x)
+    v_pu = cp(T.uq2[:].bitcast(dt.uint32), T.uq[:].bitcast(dt.uint32).indirect(off[:, 16:24]), v_qu, v_lu)
+    x = place(2, x)
+    c2 = ts(T.c2[:], T.lidx[:], line, A.is_equal, -1.0 / 32, A.mult, i_lx, v_p2)
+    x = tests(3, x)
     v_qx = [qz(blk(T.xq, 0), blk(T.xp, 0), blk(T.xin, 0, 512), k_x)]
-    x = st_place(2, x)
+    v_ww = tt(T.ww[:], left(T.d0, 2), right(T.d0, 2), A.add, x)
+    x = place(3, x)
     v_qx.append(qz(blk(T.xq, 1), blk(T.xp, 1), blk(T.xin, 1, 512)))
     p_s, p_d = products(v_qx, v_pu, a_pu)
-    act(T.fd[:, 1:256:2], T.ttin[:], AF.Identity, -1.0 / 32, 2.0, i_tt)
-    act(T.fd[:, 257:512:2], T.ttin[:], AF.Identity, -1.0 / 32, 2.0)
-    a_g16 = act(T.g16[:], T.ttin[:], AF.Identity, -1.0 / 32, 2.0)
-    a_t2 = [half_t(b, p_d) for b in range(2)]
-    x = st_fit(2, x)
-    v_li = ts(off[:, 24:40], T.io32[:, 24:40], i4, A.add, None, None, i_li)
-    y = st_free(2, x)
-    st_bad(2)
-    x = st_u(3, y, a_th[3])
-    z = gap_min(p_s)
-    x = st_place(3, x)
-    a_qp = act(T.qp[:], T.o3[:].indirect(off[:, 32:40]), AF.Identity, -1.0, 17.0 / 64, x, v_li)
-    z = gap_less(z)
-    x = st_fit(3, x)
-    v_gp = gap_last(z)
-    x = st_bad(3, x, a_qp)
-    a_eh = act(T.fd[:, 128:256:2], T.o3[:].indirect(off[:, 28:32]), AF.Identity, -1.0 / 256, T.cols[:, 1:2], x)
-    a_ee = act(T.fd[:, 0:128:2], T.o3[:].indirect(off[:, 24:28]), AF.Identity, 1.0 / 256, T.cols[:, 0:1])
-    a_t2 += [half_t(2, p_d)]
+    a_vh = lin(T.fd[:, 0:192:3], right(T.st, 131), -64.0 / SC, T.cols[:, 1:2], x, a_cols)
+    a_ve = lin(T.fd[:, 192:384:3], left(T.st, 131), 64.0 / SC, T.cols[:, 0:1])
+    a_t2 = [half_t(key, p_d) for key in ((0, 0), (1, 0), (0, 1), (1, 1), 2, 3)][2:]
+    y = scan(T.pi[:], left(T.st, 131), right(T.st, 131), 4.0, A.min, A.add, x)
+    x = scan(T.sg[:], left(T.st, 130), right(T.st, 130), 4.0, A.min, A.add)
+    z = gap_min(0, p_s[0])
+    tt(T.fs[:, 2:192:3], T.pi[:], T.ww[:], A.is_le, y, v_ww)
+    x = ts(T.fs[:, 1:192:3], T.sg[:], 130.0 / 64, A.is_ge, None, None, x)
+    z0 = gap_less(0, z)
+    z = gap_min(1, p_s[1])
+    v_tab = scan(blk(T.tab, 0, 192), T.fs[:], blk(T.fd, 0, 192), 0.0, A.mult, A.add, x, a_vh)
+    z = gap_less(1, z)
+    c2 = ts(T.c2[:, 15:256:16], T.lidx[:, 0:256:16], line, A.is_equal, None, None, c2)
+    v_tae = scan(blk(T.tab, 1, 192), T.fs[:], blk(T.fd, 1, 192), 0.0, A.mult, A.add, a_ve)
+    v_gp = scan(T.gs[:], T.c2[:], T.dd[:], 1.0, A.add, A.max, z, c2)
     v_ne = gap_mask(v_gp, a_g16)
-    v_p2 = tr(T.pp[:, 64:96], T.ppin[:, 64:96], i_p2)
-    v_ff = tt(T.ff[:], T.o3[:].indirect(off[:, 24:32]), T.qp[:], A.max, x)
-    cp(off[:, 40:48], T.pp[:, 64:72], v_p2)
-    act(T.fd[:, 256:384:2], T.ff[:, 0:64], AF.Identity, 1.0 / 256, -64.0 / SC, v_ff)
-    a_fl = act(T.fd[:, 384:512:2], T.ff[:, 64:128], AF.Identity, -1.0 / 256, -49.0 / SC)
-    a_t2 += [half_t(3, p_d)]
-    x = tt(T.gg[:], T.ff[:, 0:64], T.ff[:, 64:128], A.add, v_ff)
-    cp(T.w8[:, 1:128:2], T.w8in[:, 1:128:2], i_w8)
-    x = ts(T.fs[:, 1:128:2], T.gg[:], 15.0 / 64, A.is_le, None, None, x)
-    ts(T.w8[:, 0:128:2], T.w8in[:, 0:128:2], T.cols[:, 2:3], A.add, None, None, a_cols)
-    v_tab = scan(blk(T.tab, 1), T.fs[:], blk(T.fd, 1), 0.0, A.mult, A.add, x, a_eh)
-    v_tae = scan(blk(T.tab, 0), T.fs[:], blk(T.fd, 0), 0.0, A.mult, A.add, a_ee)
-    scan(blk(T.tab, 2), T.fs[:], blk(T.fd, 2), 0.0, A.mult, A.add, a_fl)
-    v_taf = scan(blk(T.tab, 3), T.fs[:], blk(T.fd, 3), 0.0, A.mult, A.add)
 
-    sent = [0]
+    def covered(lists, n, tmp, out, *d):
+        ts(tmp[:, 0:8:2], lists[0], T.cols[:, 3:4], A.subtract, None, None, *d)
+        x = ts(tmp[:, 1:8:2], lists[1], T.cols[:, 3:4], A.subtract, None, None)
+        scan(out[:, 0:8], blk(T.up1, n, 8), tmp[:, 0:8], 0.0, A.add, A.min, x, a_m)
+        return scan(out[:, 15:7:-1], blk(T.dn1, R - n, 8), tmp[:, 7::-1], 0.0, A.add, A.max)
+
     v_qv = None
     for t in range(R):
-        peer = T.cores[rank ^ (1 << t)]
-        rid, pid, _se = topo.addr(peer)
-        eng = topo.engines(core, peer)
-        mask = sum(1 << e for e in eng)
+        last = t == R - 1
+        rid, pid, _se = topo.addr(peers[t])
+        eng = allowed[t]
+        mask = bits(eng)
         lo = 128 + K * t
+        oe = blk(T.oe, t, 8)
         if t > 0:
-            p_s, p_d = products(v_qx)
-            a_t2 = [half_t(b, p_d) for b in range(4)]
-            v_gp = gap_last(gap_less(gap_min(p_s)))
-            v_ne = gap_mask(v_gp)
-            v_tab = v_ne
-        x = scan(T.se[:, K:2 * K], T.ne[:, 0:K], T.tab[:, 129:256:2], 4.0, A.mult, A.max, v_ne, v_tab)
-        y = scan(T.se[:, 0:K], T.ne[:, 0:K], T.tab[:, 1:128:2], 4.0, A.mult, A.max, v_tae)
-        v_off = ts(T.oeh[:, 4:8], T.se[:, K + 15:2 * K:16], gp, A.subtract, SC, A.mult, x)
-        v_ofe = ts(T.oeh[:, 0:4], T.se[:, 15:K:16], gp, A.subtract, SC, A.mult, y)
+            a_t2 = [half_t(key, p_d) for key in ((0, 0), (1, 0), (0, 1), (1, 1), 2, 3)][2:]
+            z0 = gap_less(0, gap_min(0, p_s[0]))
+            z = gap_min(1, p_s[1])
+            z0 = gap_last(0, z0)
+            z = gap_less(1, z)
+            v_ne = gap_mask(gap_last(1, z0, z))
+        x = scan(T.se[:, K:2 * K], T.ne[:], T.tab[:, 2:192:3], 4.0, A.mult, A.max, v_ne, v_tab)
+        y = scan(T.se[:, 0:K], T.ne[:], T.tab[:, 194:384:3], 4.0, A.mult, A.max, v_tae)
+        e_list, h_list = T.oe[:, 8 * t:8 * t + 4], T.oe[:, 8 * t + 4:8 * t + 8]
+        v_off = ts(h_list, T.se[:, K + 15:2 * K:16], gp, A.subtract, SC, A.mult, x)
+        v_ofe = ts(e_list, T.se[:, 15:K:16], gp, A.subtract, SC, A.mult, y)
+        wait("g", v_ofe)
+        g.remote_dma(blk(T.lb, t, 8), oe, T.sem["ac%d" % t], T.sem.sent, pid, rid, mask)
 
         def win(b):
-            return T.t2[:, PL * b:PL * b + 257]
+            return blk(T.t2, b, PL)
 
-        a_n = [None] + [act(blk(T.nn, b, K), win(b).indirect(T.oeh[:, 4:8]), AF.Copy, None, None, v_off, a_t2[b])
+        a_n = [None] + [act(blk(T.nn, b, K), win(b).indirect(h_list), AF.Copy, None, None, v_off, a_t2[b])
                         for b in range(1, 4)]
-        v_sf = scan(T.sf[:], T.ne[:], T.tab[:, 257:512:2], 4.0, A.mult, A.max, v_taf)
-        a_n[0] = cp(T.nn[:, 0:K], win(0).indirect(T.oeh[:, 4:8]), v_off, a_t2[0])
-        bd, lb = T["bd%d" % t], T["lb%d" % t]
-        v_bd = ts(bd[:], T.sf[:, 15:128:16], gp, A.subtract, SC, A.mult, v_sf)
-        wait("g", v_bd)
-        g.remote_dma(lb[:], bd[:], T.sem["ac%d" % t], T.sem.sent, pid, rid, mask)
-        for b in (1, 0, 2, 3):
-            x = tt(T.zt[:, b:256:4], win(b).indirect(T.oeh[:, 0:4]), blk(T.nn, b, K), A.add, a_n[b], v_ofe)
+        a_n[0] = cp(T.nn[:, 0:K], win(0).indirect(h_list), v_off, a_t2[0])
+        for b in range(4):
+            x = tt(T.zt[:, b:256:4], win(b).indirect(e_list), blk(T.nn, b, K), A.add, a_n[b], v_ofe)
         zq, zp = (T["zq%d" % t], T["zp%d" % t]) if t else (T.lq, T.lp)
         v_qz = qz(zq[:, 0:128], zp[:, 0:128], T.zt[:], x)
         wait("g", v_qz)
         g.remote_dma(T.lq[:, lo:lo + K].bitcast(dt.uint8), zq[:, 0:K].bitcast(dt.uint8), T.sem["az%d" % t], T.sem.sent, pid, rid, mask)
         g.remote_dma(T.lp[:, lo:lo + K], zp[:, 0:K], T.sem["az%d" % t], T.sem.sent, pid, rid, mask)
         sent[0] += 3 * len(eng)
-        a_tf = [act(blk(T.tf, b, C), bank(1 + b, C), AF.Copy, None, None) for b in range(2)]
+        keys = ((0, 0), (0, 1), (1, 0)) if last else ((0, 0), (0, 1), (1, 0), (1, 1))
+        a_tf = [act(blk(T.tf, 2 * b + h), bank(dbank[b, h], 128), AF.Copy, None, None) for b, h in keys][-1]
         if t == 0:
             ms(T.ha[:, 0:258:2], 0.0)
-            v_hz = ms(T.hb[:, 0:258:2], 0.0)
+            ms(T.hb[:, 0:258:2], 0.0)
+            cp(off[:, 24:32], T.pp[:, 96:104])
+            x = [ms(T.w8[:, 2 * k + 1:128:8], 96.0 - 32 * k) for k in range(4)][3]
+            v_w8 = ts(T.w8[:, 0:128:2], T.w8[:, 1:128:2], T.cols[:, 2:3], A.add, None, None, x)
+            for h in range(2):
+                lin(T.j8[:, h:128:2], T.lidx[:, 0:256:4], -1.0, 15.0 + h)
+            fill(T.up1[:, 0:32:2], 16, 1000.0)
+            fill(T.dn1[:, 0:32:2], 16, -1000.0)
+            act(T.up1[:, 1:32:2], T.lm[:], AF.Copy, None, None, k_m)
+            a_m = act(T.dn1[:, 1:32:2], T.lm[:, 15::-1], AF.Copy, -1.0, None)
         if t == 1:
             v_qv = qz(T.vq[:], T.vp[:], T.vin[:], k_v)
-        if t == R - 1:
-            x = ts(T.ob1[:], bd[:].indirect(off[:, 40:41]), 0.0, A.is_lt, 65.0, A.mult)
-            x = tt(T.ob2[:], bd[:].indirect(off[:, 40:41]), T.ob1[:], A.add, x)
-            x = ts(T.ob3[:], T.ob2[:], -1.0, A.add, None, None, x)
-            dma("s", "dout", T.ob[:], T.ob3[:, 0:8], x)
-        x = tt(T.nf[:], lb[:].indirect(off[:, 40:48]), T.j8[:], A.is_gt, ("ac%d" % t, len(eng)), i_j8)
+        if last:
+            x = covered((e_list, h_list), R, T.of, T.ob1)
+            ts(T.ob2[:, 0:8:2], T.ob1[:, 8:16:2], -1.0, A.max, None, None, x)
+            x = ts(T.ob2[:, 1:8:2], T.ob1[:, 1:8:2], -1.0, A.max, None, None)
+            dma("s", "dout", T.ob[:], T.ob2[:], x)
+        x = covered((blk(T.lb, 2 * t, 4), blk(T.lb, 2 * t + 1, 4)), t, T.lf, T.bb, ("ac%d" % t, len(eng)))
+        x = tt(T.nf[:], T.bb[:].indirect(off[:, 24:32]), T.j8[:], A.is_lt, x, v_w8)
         x = scan(T.cs[:], T.nf[:], T.w8[:], 128.0, A.mult, A.max, x)
-        v_lc = cp(T.lc[:], T.cs[:, 7:128:8], x)
-        hk = (0, 7, 5, 6)
-        p_h = [mm(bank(hk[b], 128), blk(T.wq, b), blk(T.wp, b), T.lq[:, lo - K:lo + K], T.lp[:, lo - K:lo + K],
-                  k_w, v_qz, ("az%d" % t, 2 * len(eng))) for b in range(4)]
-        v_h = [ts(T.ha[:, 128 * b + 1:128 * b + 128:2], bank(hk[b], 128, K), 0.03125, A.mult, None, None, p_h[b]) for b in range(2)]
-        a_h = [act(T.hb[:, 128 * b + 1:128 * b + 128:2], bank(hk[2 + b], 128, K), AF.Copy, 0.03125, None, p_h[2 + b], v_hz)
-               for b in range(2)]
-        a_g = [act(blk(T.g2, b, C), T.hb[:, 128 * b:128 * b + 129].indirect(T.lc[:]), AF.Copy, None, None, a_h[b], v_lc)
-               for b in range(2)]
-        for b in range(2):
-            tt(T.xn[:, b:1024:4], T.ha[:, 128 * b:128 * b + 129].indirect(T.lc[:]), blk(T.tf, b, C), A.add,
-               v_h[b], v_lc, a_tf[b])
-        tt(T.xn[:, 2:1024:4], blk(T.g2, 0, C), bank(3, C), A.add, a_g[0])
-        x = [tt(T.xn[:, 512 * h + 3:512 * h + 512:4], blk(T.g2, 2 + h), bank(4, 128 * h + 128, 128 * h), A.add, a_g[1])
-             for h in range(2)]
-        v_qx = [qz(blk(T.xq, h), blk(T.xp, h), blk(T.xn, h, 512), x[h]) for h in range(2)]
+        v_lc = cp(T.lc[:], T.cs[:, 127:6:-8], x)
+        hk = {2: 0, 0: 7, 3: 1, 1: 5}
+        p_h = {b: mm(bank(hk[b], 128), blk(T.wq, b), blk(T.wp, b), T.lq[:, lo - K:lo + K], T.lp[:, lo - K:lo + K],
+                     k_w, v_qz, a_tf, ("az%d" % t, 2 * len(eng))) for b in hk}
+
+        def h_out(b):
+            return (T.ha, T.hb)[b // 2][:, 128 * (b % 2) + 1:128 * (b % 2) + 128:2]
+
+        def h_pick(b, a, n):
+            return (T.ha, T.hb)[b // 2][:, 128 * (b % 2):128 * (b % 2) + 129].indirect(T.lc[:, a:a + n])
+
+        def new(b, h, n=1):
+            return T.xn[:, 512 * h + b:512 * (h + n):4]
+
+        def quant(h, *d):
+            return qz(blk(T.xq, h), blk(T.xp, h), blk(T.xn, h, 512), *d)
+
+        def add(b, h, *d):
+            return tt(new(b, h), blk(T.g2, 2 * b - 4 + h), bank(1 + b, 128 * h + 128, 128 * h), A.add, *d)
+
+        if t == 0:
+            k_v = dma("s", "dv", T.vin[:], T.v[:], p_h[2])
+        a_h2 = act(h_out(2), bank(hk[2], 128, K), AF.Copy, 0.03125, None, p_h[2], v_w8)
+        v_h0 = ts(h_out(0), bank(hk[0], 128, K), 0.03125, A.mult, None, None, p_h[0])
+        v_h3 = ts(h_out(3), bank(hk[3], 128, K), 0.03125, A.mult, None, None, p_h[3])
+        if not last:
+            a_g2 = act(blk(T.g2, 0, C), h_pick(2, 0, 16), AF.Copy, None, None, a_h2, v_lc)
+            a_h1 = act(h_out(1), bank(hk[1], 128, K), AF.Copy, 0.03125, None, p_h[1])
+            a_g3 = act(blk(T.g2, 1, C), h_pick(3, 0, 16), AF.Copy, None, None, v_h3)
+            tt(new(0, 0, 2), h_pick(0, 0, 16), blk(T.tf, 0, C), A.add, v_h0, v_lc, a_tf)
+            tt(new(1, 0, 2), h_pick(1, 0, 16), blk(T.tf, 1, C), A.add, a_h1)
+            add(2, 0, a_g2)
+            x = add(3, 0, a_g3)
+            add(2, 1)
+            v_qx = [quant(0, x)]
+            v_qx.append(quant(1, add(3, 1)))
+            p_s, p_d = products(v_qx)
+            continue
+        a_g = {(2, 0): act(blk(T.g2, 0), h_pick(2, 0, 8), AF.Copy, None, None, a_h2, v_lc)}
+        a_h1 = act(h_out(1), bank(hk[1], 128, K), AF.Copy, 0.03125, None, p_h[1])
+        a_g[3, 0] = act(blk(T.g2, 2), h_pick(3, 0, 8), AF.Copy, None, None, v_h3)
+        a_g[2, 1] = act(blk(T.g2, 1), h_pick(2, 8, 8), AF.Copy, None, None)
+        a_g[3, 1] = act(blk(T.g2, 3), h_pick(3, 8, 8), AF.Copy, None, None)
+        a_g[1, 1] = act(blk(T.g2, 4), h_pick(1, 8, 8), AF.Copy, None, None, a_h1)
+        tt(new(0, 0), h_pick(0, 0, 8), blk(T.tf, 0), A.add, v_h0, v_lc, a_tf)
+        tt(new(1, 0), h_pick(1, 0, 8), blk(T.tf, 2), A.add, a_h1)
+        add(2, 0, a_g[2, 0])
+        x = add(3, 0, a_g[3, 0])
+        tt(new(0, 1), h_pick(0, 8, 8), blk(T.tf, 1), A.add)
+        v_qx = [quant(0, x)]
+        add(2, 1, a_g[2, 1])
+        add(3, 1, a_g[3, 1])
+        v_qx.append(quant(1, tt(new(1, 1), blk(T.g2, 4), bank(dbank[1, 1], 128), A.add, a_g[1, 1])))
 
     p_y = [mm(bank(7 * h, 128), T.vq[:], T.vp[:], blk(T.xq, h), blk(T.xp, h), v_qv, v_qx[h]) for h in range(2)]
-    y = act(T.ys[:, 0:128], bank(0, 128), AF.Copy, None, None, p_y[0])
-    x = cp(T.ys[:, 128:256], bank(7, 128), p_y[1])
-    dma("s", "dout", T.oc[:], T.xq[:].bitcast(dt.uint8), v_qx[1])
+    y = [act(T.ys[:, 0:128], bank(0, 128), AF.Copy, None, None, p_y[0]), cp(T.ys[:, 128:256], bank(7, 128), p_y[1])]
+    for h in range(2):
+        dma("s", "dout", blk(T.oc, h, 512), blk(T.xq, h).bitcast(dt.uint8), v_qx[h])
+        dma("s", "dout", blk(T.y, h), blk(T.ys, h), y[h])
     for k in range(4):
-        dma("a", "dout", T.osc[4 * k:4 * k + 4, :], T.xp[32 * k:32 * k + 4, :], v_qx[1])
-    last = dma("s", "dout", T.y[:], T.ys[:], x, y)
+        end = dma("a", "dout", T.osc[4 * k:4 * k + 4, :], T.xp[32 * k:32 * k + 4, :], v_qx[1])
     wait("g", ("sent", sent[0]), ("sg", cnt["g"]), ("sp", cnt["p"]), ("sv", cnt["v"]), ("sa", cnt["a"]))
-    wait("s", last)
+    wait("s", end)

@@ -18,7 +18,7 @@ SCRATCH = {
     "vq": sb(128, X4), "vp": sb(128, U8), "eq": sb(512, X4), "ep": sb(512, U8),
     "xq": sb(256, X4), "xp": sb(256, U8), "xn": sb(1024, BF),
     "lq": sb(LW, X4), "lp": sb(LW, U8), "zt": sb(512, BF),
-    "ebuf": sb(528, BF), "ones": sb(128, BF),
+    "ebuf": sb(528, BF), "ones": sb(136, BF),
     "ppin": sb(128, F32), "pp": sb(128, F32), "io32": sb(16, F32), "off": sb(32, U16),
     "tl": sb(128, BF), "lidx": sb(256, BF), "k0": sb(128, BF), "kj": sb(96, BF),
     "c1": sb(128, BF), "c2": sb(256, BF), "g16": sb(64, BF), "j8": sb(128, F32), "w8": sb(128, BF),
@@ -136,59 +136,70 @@ def rank_program(g, core, T, topo):
 
     off = T.off
     peers = [T.cores[rank ^ (1 << t)] for t in range(R)]
-    m_bl = ms(T.blrow[:], 0)
-    k_bl = dma("s", "dbl", T.blrow[0:128:32, :], T.bl[:], m_bl)
+    for n in range(4):
+        k_bl = dma("sa"[n % 2], "dbl", T.blrow[32 * n + 31:32 * n + 32, :], T.bl[32 * n:32 * n + 32, :])
     k_u = dma("s", "du", T.uin[:], T.u[:])
     k_x = dma("s", "dx", T.xin[:], T.x[:])
     dma("s", "dw", T.wq[:].bitcast(dt.uint8), T.wc[:], k_u)
     k_w = dma("s", "dw", T.wp[:], T.ws[:])
 
-    m_one = ms(T.ones[:], 1.0)
     m_e = ms(T.ebuf[:], 0.0)
+    m_one = ms(T.ones[:], 1.0)
     i_pp = iota(T.ppin[:, 0:32], [[0, 2], [1, 4], [16, 4]], 0)
     i_bl = iota(T.io32[:, 0:8], [[4, 4], [64, 2]], 0)
     wait("g", m_e)
-    i_e = done("g", g.affine_select(T.ebuf[:, 3:515:4], T.ones[:], [[-1, 128]], A.is_equal, 0.0, 0, 1))
-    i_tl = iota(T.tl[:], [[0, 4], [1, 16], [0, 2]], 0)
-    iota(T.ppin[:, 32:64], [[0, 16], [-2, 2]], 1)
-    i_lk = iota(T.io32[:, 8:16], [[32, 4], [0, 2]], -48)
+    i_e = done("g", g.affine_select(T.ebuf[:, 3:515:4], T.ebuf[:, 3:515:4], [[-1, 128]], A.not_equal, 1.0, 0, 1))
+    i_t0 = iota(T.tl[:, 0:32], [[1, 16], [0, 2]], 0)
+    i_lk = iota(T.ppin[:, 32:64], [[0, 16], [-64, 2]], 32)
+    i_tl = iota(T.tl[:, 32:128], [[0, 3], [1, 16], [0, 2]], 0)
     iota(T.ppin[:, 64:96], [[0, 2], [1, 16]], 0)
     i_p2 = iota(T.ppin[:, 96:128], [[0, 4], [-2, 4], [7, 2]], 7)
     i_lx = iota(T.lidx[:], [[1, 16], [0, 16]], 0)
 
-    fill(T.d0[:, 0:512:4], 128, -100.0, m_one)
+    a_c1 = fill(T.c1[:], 128, 0.0, m_one)
+    fill(T.d0[:, 0:512:4], 128, -100.0)
     fill(T.st[:, 3:128:4], 32, 49.0 / 64)
+    fill(T.c1[:, 0:128:16], 8, BIG, a_c1)
     fill(T.l0[:, 0:192:2], 96, 0.0)
     fill(T.fs[:, 0:192:3], 64, 0.0)
     fill(T.fd[:, 1:384:3], 128, 0.0)
     for b in range(4):
         fill(T.t2[:, PL * b:PL * b + Z0], Z0, 0.0)
-    m_c1 = ms(T.c1[:], 0.0)
-    ms(T.zt[:, 256:512], 0.0)
-    ms(T.dd[:, 127:256:128], 0.0)
-    ms(T.c1[:, 0:128:16], BIG, m_c1)
+    for a in range(0, 128, 32):
+        ms(T.blrow[a:a + 31, :], 0)
     v_pp = tr(T.pp[:, 0:32], T.ppin[:, 0:32], i_pp)
+    ms(T.zt[:, 256:512], 0.0)
+
+    def unit(b):
+        return qz(blk(T.eq, b), blk(T.ep, b), T.ebuf[:, 3 - b:515 - b], i_e)
+
+    v_e = [unit(0)]
     v_lb = ts(off[:, 0:8], T.io32[:, 0:8], T.pp[:, 0:1], A.add, None, None, v_pp, i_bl)
-    v_e = [qz(blk(T.eq, b), blk(T.ep, b), T.ebuf[:, 3 - b:515 - b], i_e) for b in range(4)]
+    v_e.append(unit(1))
 
     t32 = T.tl[:, 0:32]
-    a_ab = act(blk(T.k0, 3, 32), t32, AF.Abs, 1.0 / 64, -7.5 / 64, i_tl)
+    a_lk = lin(T.io32[:, 8:16], T.tl[:, 0:8], 1.0, -1.5, i_t0)
+    a_ab = act(blk(T.k0, 3, 32), t32, AF.Abs, 1.0 / 64, -7.5 / 64)
     lin(T.st[:, 2:128:4], t32, 1.0 / 64, 48.0 / 64)
     lin(blk(T.k0, 0, 32), t32, 1.0 / 64, 48.0 / 64)
     lin(blk(T.k0, 1, 32), t32, -1.0 / 64, -48.0 / 64)
-    lin(blk(T.k0, 2, 32), blk(T.k0, 3, 32), 1.0, -55.5 / 64, a_ab)
-    a_k0 = lin(T.kj[:], T.tl[:, 0:96], 1.0 / 64, -63.0 / 64)
-    lin(T.l1[:, 0:192:2], T.tl[:, 0:96], 1.0 / 64, 1.0 / 64)
+    a_k0 = lin(blk(T.k0, 2, 32), blk(T.k0, 3, 32), 1.0, -55.5 / 64, a_ab)
+    a_kj = lin(T.kj[:], T.tl[:, 32:128], 1.0 / 64, -63.0 / 64, i_tl)
+    lin(T.l1[:, 0:192:2], T.tl[:, 32:128], 1.0 / 64, 1.0 / 64)
 
     v_bt = ts(T.bt[:], T.blrow[:].indirect(off[:, 0:8]), 1.0 / 64, A.mult, -63.0 / 64, A.add, k_bl, v_lb)
     x = tr(T.pp[:, 32:64], T.ppin[:, 32:64], i_lk)
-    v_an = tr(T.an[:], T.bt[:], v_bt)
-    v_lk = ts(off[:, 8:16], T.io32[:, 8:16], T.pp[:, 32:33], A.mult, 48.0, A.add, x)
     v_lu = ts(off[:, 16:24], T.tl[:, 0:16:2], 16.0, A.mult, None, None)
-    a_mf = lin(blk(T.lm, R, 4), T.an[:, 0:128:32], 64.0, 62.0, v_an)
-    a_n = act(T.d0[:, 1:512:4], T.an[:].indirect(off[:, 8:16]), AF.Copy, None, None, v_lk)
-    a_n3 = lin(T.d0[:, 3:512:4], T.d0[:, 1:512:4], -1.0, -63.0 / 64, a_n)
-    a_th = act(T.l1[:, 1:192:2], T.d0[:, 129:512:4], AF.Copy, -1.0, None)
+    v_an = tr(T.an[:], T.bt[:], v_bt)
+    v_lk = ts(off[:, 8:16], T.io32[:, 8:16], T.pp[:, 32:33], A.mult, 48.0 + 31, A.add, x, a_lk)
+    v_e.append(unit(2))
+    k_0, k_1 = T.an[:].indirect(off[:, 8:10]), T.an[:].indirect(off[:, 10:16])
+    a_mf = lin(blk(T.lm, R, 4), T.an[:, 31:128:32], 64.0, 62.0, v_an)
+    act(T.d0[:, 1:128:4], k_0, AF.Copy, None, None, v_lk)
+    a_n0 = lin(T.d0[:, 3:128:4], k_0, -1.0, -63.0 / 64)
+    a_th = act(T.l1[:, 1:192:2], k_1, AF.Copy, -1.0, None)
+    act(T.d0[:, 129:512:4], k_1, AF.Copy, None, None)
+    a_n1 = lin(T.d0[:, 131:512:4], T.l1[:, 1:192:2], 1.0, -63.0 / 64, a_th)
 
     allowed = [topo.engines(core, p) for p in peers]
     narrow = min(allowed, key=len)
@@ -214,7 +225,7 @@ def rank_program(g, core, T, topo):
 
     def tests(s, *d):
         tt(sl(T.st, s, 0), sl(T.st, s, 2), lanes(T.l1, s), A.is_gt, *d)
-        tt(sl(T.st, s, 1), sl(T.st, s, 2), sl(T.d0, s, 1), A.add)
+        tt(sl(T.st, s, 1), sl(T.st, s, 2), lanes(T.l1, s), A.subtract)
         return tt(sl(T.d0, s, 2), sl(T.st, s, 2), lanes(T.lim, s), A.is_le, v_lim)
 
     def place(s, *d):
@@ -226,26 +237,12 @@ def rank_program(g, core, T, topo):
     def right(buf, a):
         return buf[:, a + 508:a + 3:-8]
 
-    dbank = {(0, 0): 1, (0, 1): 5, (1, 0): 2, (1, 1): 6}
-
-    def score(h, *d):
-        return mm(bank(7 * h, 128), T.uq2[:], T.up2[:], blk(T.xq, h), blk(T.xp, h), *d)
-
     def products(qx, *d):
-        s, p = [], {}
-        for h in range(2):
-            s.append(score(h, qx[h], *d))
-            for b in range(2):
-                p[b, h] = mm(bank(dbank[b, h], 128), blk(T.eq, b), blk(T.ep, b), blk(T.xq, h), blk(T.xp, h), v_e[b])
-        for b in range(2, 4):
-            p[b] = mm(bank(1 + b, C), blk(T.eq, b), blk(T.ep, b), T.xq[:], T.xp[:], v_e[b])
-        return s, p
+        s = [mm(bank(7 * h, 128), T.uq2[:], T.up2[:], blk(T.xq, h), blk(T.xp, h), qx[h], *d) for h in range(2)]
+        return s, [mm(bank(1 + b, C), blk(T.eq, b), blk(T.ep, b), T.xq[:], T.xp[:], v_e[b]) for b in range(4)]
 
-    def half_t(key, p):
-        if key in dbank:
-            a = PL * key[0] + Z0 + 128 * key[1]
-            return act(T.t2[:, a:a + 128], bank(dbank[key], 128), AF.Copy, 0.5, None, p[key])
-        return act(T.t2[:, PL * key + Z0:PL * key + PL], bank(1 + key, C), AF.Copy, 0.5, None, p[key])
+    def half_t(b, p):
+        return act(T.t2[:, PL * b + Z0:PL * b + PL], bank(1 + b, C), AF.Copy, 0.5, None, p[b])
 
     def gap_min(h, *d):
         return scan(blk(T.mm, h), T.c1[:], bank(7 * h, 128), 0.0, A.add, A.min, *d)
@@ -253,26 +250,27 @@ def rank_program(g, core, T, topo):
     def gap_less(h, *d):
         return tt(T.dd[:, 128 * h:128 * h + 127], bank(7 * h, 128, 1), T.mm[:, 128 * h:128 * h + 127], A.is_lt, *d)
 
-    def gap_last(h, *d):
-        return scan(blk(T.gs, h), blk(T.c2, h), blk(T.dd, h), T.gs[:, 127:128] if h else 1.0, A.add, A.max, *d)
+    def gap_last(*d):
+        return scan(T.gs[:], T.c2[:], T.dd[:], 1.0, A.add, A.max, *d)
 
     gp = T.gs[:, 255:256]
 
     def gap_mask(*d):
         return ts(T.ne[:], T.g16[:], gp, A.not_equal, None, None, *d)
 
-    k_0 = T.an[:].indirect(off[:, 8:10])
     tt(sl(T.st, 0, 0), k_0, blk(T.k0, 1, 32), A.is_gt, v_an, v_lk, a_k0)
     tt(sl(T.st, 0, 1), k_0, blk(T.k0, 0, 32), A.add)
     x = tt(sl(T.d0, 0, 2), k_0, blk(T.k0, 2, 32), A.is_le)
-    y = tt(T.l0[:, 1:192:2], T.an[:].indirect(off[:, 10:16]), T.kj[:], A.is_le)
-    x = place(0, x, a_n3)
+    y = tt(T.l0[:, 1:192:2], k_1, T.kj[:], A.is_le, a_kj)
+    x = place(0, x, a_n0)
+    v_qu = qz(T.uq[:], T.up[:], T.uin[:], k_u)
     v_lim = scan(T.lim[:], T.l0[:], T.l1[:], 0.0, A.mult, A.add, y, a_th)
     x = tests(1, x)
-    v_qu = qz(T.uq[:], T.up[:], T.uin[:], k_u)
     a_pu = act(T.up2[:], T.up[:].indirect(off[:, 16:24]), AF.Copy, None, None, v_qu, v_lu)
-    x = place(1, x)
+    v_pu = cp(T.uq2[:].bitcast(dt.uint32), T.uq[:].bitcast(dt.uint32).indirect(off[:, 16:24]), v_qu, v_lu)
+    x = place(1, x, a_n1)
     v_p2 = tr(T.pp[:, 64:128], T.ppin[:, 64:128], i_p2)
+    v_e.append(unit(3))
     line = T.pp[:, 64:65]
     lin(T.cols[:, 0:1], line, 16.0 / SC, (Z0 - 64.0) / SC, v_p2)
     lin(T.cols[:, 1:2], line, 16.0 / SC, (Z0 + 64.0) / SC)
@@ -280,33 +278,34 @@ def rank_program(g, core, T, topo):
     a_cols = lin(T.cols[:, 3:4], line, 16.0, float(Z0))
     for h in range(2):
         lin(T.fd[:, 192 * h + 2:192 * h + 192:3], T.tl[:, 0:128:2], -1.0 / 32 - 1.0 / SC, 2.0 + 15.0 / SC)
+    fill(T.dd[:, 127:256:128], 2, 0.0)
     a_g16 = lin(T.g16[:], T.tl[:, 0:128:2], -1.0 / 32, 2.0)
     x = tests(2, x)
-    v_pu = cp(T.uq2[:].bitcast(dt.uint32), T.uq[:].bitcast(dt.uint32).indirect(off[:, 16:24]), v_qu, v_lu)
-    x = place(2, x)
-    c2 = ts(T.c2[:], T.lidx[:], line, A.is_equal, -1.0 / 32, A.mult, i_lx, v_p2)
-    x = tests(3, x)
     v_qx = [qz(blk(T.xq, 0), blk(T.xp, 0), blk(T.xin, 0, 512), k_x)]
-    v_ww = tt(T.ww[:], left(T.d0, 2), right(T.d0, 2), A.add, x)
-    x = place(3, x)
+    x = place(2, x)
     v_qx.append(qz(blk(T.xq, 1), blk(T.xp, 1), blk(T.xin, 1, 512)))
     p_s, p_d = products(v_qx, v_pu, a_pu)
-    a_vh = lin(T.fd[:, 0:192:3], right(T.st, 131), -64.0 / SC, T.cols[:, 1:2], x, a_cols)
+    x = tests(3, x)
+    c2 = ts(T.c2[:], T.lidx[:], line, A.is_equal, -1.0 / 32, A.mult, i_lx, v_p2)
+    c2 = act(T.c2[:, 15:256:16], T.c2[:, 0:256:16], AF.Copy, -32.0, None, c2)
+    x3 = place(3, x)
+    z0 = gap_min(0, p_s[0])
+    a_vh = lin(T.fd[:, 0:192:3], right(T.st, 131), -64.0 / SC, T.cols[:, 1:2], x3, a_cols)
     a_ve = lin(T.fd[:, 192:384:3], left(T.st, 131), 64.0 / SC, T.cols[:, 0:1])
-    a_t2 = [half_t(key, p_d) for key in ((0, 0), (1, 0), (0, 1), (1, 1), 2, 3)][2:]
-    y = scan(T.pi[:], left(T.st, 131), right(T.st, 131), 4.0, A.min, A.add, x)
+    a_t2 = [half_t(b, p_d) for b in range(4)]
+    v_ww = tt(T.ww[:], left(T.d0, 2), right(T.d0, 2), A.add, x)
+    y = scan(T.pi[:], left(T.st, 131), right(T.st, 131), 4.0, A.min, A.add, x3)
     x = scan(T.sg[:], left(T.st, 130), right(T.st, 130), 4.0, A.min, A.add)
-    z = gap_min(0, p_s[0])
+    z1 = gap_min(1, p_s[1])
     tt(T.fs[:, 2:192:3], T.pi[:], T.ww[:], A.is_le, y, v_ww)
     x = ts(T.fs[:, 1:192:3], T.sg[:], 130.0 / 64, A.is_ge, None, None, x)
-    z0 = gap_less(0, z)
-    z = gap_min(1, p_s[1])
+    gap_less(0, z0)
+    z = gap_less(1, z1)
     v_tab = scan(blk(T.tab, 0, 192), T.fs[:], blk(T.fd, 0, 192), 0.0, A.mult, A.add, x, a_vh)
-    z = gap_less(1, z)
-    c2 = ts(T.c2[:, 15:256:16], T.lidx[:, 0:256:16], line, A.is_equal, None, None, c2)
+    v_gp = gap_last(z, c2)
     v_tae = scan(blk(T.tab, 1, 192), T.fs[:], blk(T.fd, 1, 192), 0.0, A.mult, A.add, a_ve)
-    v_gp = scan(T.gs[:], T.c2[:], T.dd[:], 1.0, A.add, A.max, z, c2)
     v_ne = gap_mask(v_gp, a_g16)
+    cp(off[:, 24:32], T.pp[:, 96:104])
 
     def covered(lists, n, tmp, out, *d):
         ts(tmp[:, 0:8:2], lists[0], T.cols[:, 3:4], A.subtract, None, None, *d)
@@ -323,12 +322,9 @@ def rank_program(g, core, T, topo):
         lo = 128 + K * t
         oe = blk(T.oe, t, 8)
         if t > 0:
-            a_t2 = [half_t(key, p_d) for key in ((0, 0), (1, 0), (0, 1), (1, 1), 2, 3)][2:]
-            z0 = gap_less(0, gap_min(0, p_s[0]))
-            z = gap_min(1, p_s[1])
-            z0 = gap_last(0, z0)
-            z = gap_less(1, z)
-            v_ne = gap_mask(gap_last(1, z0, z))
+            a_t2 = [half_t(b, p_d) for b in range(4)]
+            z = [gap_min(h, p_s[h]) for h in range(2)]
+            v_ne = gap_mask(gap_last([gap_less(h, z[h]) for h in range(2)][1]))
         x = scan(T.se[:, K:2 * K], T.ne[:], T.tab[:, 2:192:3], 4.0, A.mult, A.max, v_ne, v_tab)
         y = scan(T.se[:, 0:K], T.ne[:], T.tab[:, 194:384:3], 4.0, A.mult, A.max, v_tae)
         e_list, h_list = T.oe[:, 8 * t:8 * t + 4], T.oe[:, 8 * t + 4:8 * t + 8]
@@ -351,20 +347,18 @@ def rank_program(g, core, T, topo):
         g.remote_dma(T.lq[:, lo:lo + K].bitcast(dt.uint8), zq[:, 0:K].bitcast(dt.uint8), T.sem["az%d" % t], T.sem.sent, pid, rid, mask)
         g.remote_dma(T.lp[:, lo:lo + K], zp[:, 0:K], T.sem["az%d" % t], T.sem.sent, pid, rid, mask)
         sent[0] += 3 * len(eng)
-        keys = ((0, 0), (0, 1), (1, 0)) if last else ((0, 0), (0, 1), (1, 0), (1, 1))
-        a_tf = [act(blk(T.tf, 2 * b + h), bank(dbank[b, h], 128), AF.Copy, None, None) for b, h in keys][-1]
         if t == 0:
-            ms(T.ha[:, 0:258:2], 0.0)
-            ms(T.hb[:, 0:258:2], 0.0)
-            cp(off[:, 24:32], T.pp[:, 96:104])
-            x = [ms(T.w8[:, 2 * k + 1:128:8], 96.0 - 32 * k) for k in range(4)][3]
-            v_w8 = ts(T.w8[:, 0:128:2], T.w8[:, 1:128:2], T.cols[:, 2:3], A.add, None, None, x)
-            for h in range(2):
-                lin(T.j8[:, h:128:2], T.lidx[:, 0:256:4], -1.0, 15.0 + h)
+            x = [fill(T.w8[:, 2 * k + 1:128:8], 16, 96.0 - 32 * k) for k in range(4)][3]
             fill(T.up1[:, 0:32:2], 16, 1000.0)
             fill(T.dn1[:, 0:32:2], 16, -1000.0)
             act(T.up1[:, 1:32:2], T.lm[:], AF.Copy, None, None, k_m)
             a_m = act(T.dn1[:, 1:32:2], T.lm[:, 15::-1], AF.Copy, -1.0, None)
+            for h in range(2):
+                lin(T.j8[:, h:128:2], T.lidx[:, 0:256:4], -1.0, 15.0 + h)
+            a_w8 = lin(T.w8[:, 0:128:2], T.w8[:, 1:128:2], 1.0, T.cols[:, 2:3], x)
+            fill(T.ha[:, 0:258:2], 129, 0.0)
+            a_hz = fill(T.hb[:, 0:258:2], 129, 0.0)
+        a_tf = [act(blk(T.tf, b, C), bank(1 + b, C), AF.Copy, None, None) for b in range(2)]
         if t == 1:
             v_qv = qz(T.vq[:], T.vp[:], T.vin[:], k_v)
         if last:
@@ -373,12 +367,12 @@ def rank_program(g, core, T, topo):
             x = ts(T.ob2[:, 1:8:2], T.ob1[:, 1:8:2], -1.0, A.max, None, None)
             dma("s", "dout", T.ob[:], T.ob2[:], x)
         x = covered((blk(T.lb, 2 * t, 4), blk(T.lb, 2 * t + 1, 4)), t, T.lf, T.bb, ("ac%d" % t, len(eng)))
-        x = tt(T.nf[:], T.bb[:].indirect(off[:, 24:32]), T.j8[:], A.is_lt, x, v_w8)
+        x = tt(T.nf[:], T.bb[:].indirect(off[:, 24:32]), T.j8[:], A.is_lt, x, a_w8)
         x = scan(T.cs[:], T.nf[:], T.w8[:], 128.0, A.mult, A.max, x)
         v_lc = cp(T.lc[:], T.cs[:, 127:6:-8], x)
-        hk = {2: 0, 0: 7, 3: 1, 1: 5}
+        hk = {0: 0, 2: 7, 1: 5, 3: 6}
         p_h = {b: mm(bank(hk[b], 128), blk(T.wq, b), blk(T.wp, b), T.lq[:, lo - K:lo + K], T.lp[:, lo - K:lo + K],
-                     k_w, v_qz, a_tf, ("az%d" % t, 2 * len(eng))) for b in hk}
+                     k_w, v_qz, ("az%d" % t, 2 * len(eng))) for b in hk}
 
         def h_out(b):
             return (T.ha, T.hb)[b // 2][:, 128 * (b % 2) + 1:128 * (b % 2) + 128:2]
@@ -397,42 +391,32 @@ def rank_program(g, core, T, topo):
 
         if t == 0:
             k_v = dma("s", "dv", T.vin[:], T.v[:], p_h[2])
-        a_h2 = act(h_out(2), bank(hk[2], 128, K), AF.Copy, 0.03125, None, p_h[2], v_w8)
-        v_h0 = ts(h_out(0), bank(hk[0], 128, K), 0.03125, A.mult, None, None, p_h[0])
+        v_h0 = ts(h_out(0), bank(hk[0], 128, K), 0.03125, A.mult, None, None, p_h[0], a_hz)
+        a_h2 = act(h_out(2), bank(hk[2], 128, K), AF.Copy, 0.03125, None, p_h[2])
+        a_h1 = act(h_out(1), bank(hk[1], 128, K), AF.Copy, 0.03125, None, p_h[1])
+        a_g2 = act(blk(T.g2, 0, C), h_pick(2, 0, 16), AF.Copy, None, None, a_h2, v_lc)
+        tt(new(0, 0, 2), h_pick(0, 0, 16), blk(T.tf, 0, C), A.add, v_h0, v_lc, a_tf[0])
         v_h3 = ts(h_out(3), bank(hk[3], 128, K), 0.03125, A.mult, None, None, p_h[3])
+        tt(new(1, 0, 2), h_pick(1, 0, 16), blk(T.tf, 1, C), A.add, a_h1, a_tf[1])
         if not last:
-            a_g2 = act(blk(T.g2, 0, C), h_pick(2, 0, 16), AF.Copy, None, None, a_h2, v_lc)
-            a_h1 = act(h_out(1), bank(hk[1], 128, K), AF.Copy, 0.03125, None, p_h[1])
             a_g3 = act(blk(T.g2, 1, C), h_pick(3, 0, 16), AF.Copy, None, None, v_h3)
-            tt(new(0, 0, 2), h_pick(0, 0, 16), blk(T.tf, 0, C), A.add, v_h0, v_lc, a_tf)
-            tt(new(1, 0, 2), h_pick(1, 0, 16), blk(T.tf, 1, C), A.add, a_h1)
-            add(2, 0, a_g2)
-            x = add(3, 0, a_g3)
-            add(2, 1)
-            v_qx = [quant(0, x)]
-            v_qx.append(quant(1, add(3, 1)))
+            tt(new(2, 0, 2), blk(T.g2, 0, C), bank(3, C), A.add, a_g2)
+            x = [add(3, h, a_g3) for h in range(2)]
+            v_qx = [quant(h, x[h]) for h in range(2)]
             p_s, p_d = products(v_qx)
             continue
-        a_g = {(2, 0): act(blk(T.g2, 0), h_pick(2, 0, 8), AF.Copy, None, None, a_h2, v_lc)}
-        a_h1 = act(h_out(1), bank(hk[1], 128, K), AF.Copy, 0.03125, None, p_h[1])
-        a_g[3, 0] = act(blk(T.g2, 2), h_pick(3, 0, 8), AF.Copy, None, None, v_h3)
-        a_g[2, 1] = act(blk(T.g2, 1), h_pick(2, 8, 8), AF.Copy, None, None)
-        a_g[3, 1] = act(blk(T.g2, 3), h_pick(3, 8, 8), AF.Copy, None, None)
-        a_g[1, 1] = act(blk(T.g2, 4), h_pick(1, 8, 8), AF.Copy, None, None, a_h1)
-        tt(new(0, 0), h_pick(0, 0, 8), blk(T.tf, 0), A.add, v_h0, v_lc, a_tf)
-        tt(new(1, 0), h_pick(1, 0, 8), blk(T.tf, 2), A.add, a_h1)
-        add(2, 0, a_g[2, 0])
-        x = add(3, 0, a_g[3, 0])
-        tt(new(0, 1), h_pick(0, 8, 8), blk(T.tf, 1), A.add)
+        a_g3 = [act(blk(T.g2, 2 + h), h_pick(3, 8 * h, 8), AF.Copy, None, None, v_h3) for h in range(2)]
+        add(2, 0, a_g2)
+        x = add(3, 0, a_g3[0])
+        add(2, 1)
         v_qx = [quant(0, x)]
-        add(2, 1, a_g[2, 1])
-        add(3, 1, a_g[3, 1])
-        v_qx.append(quant(1, tt(new(1, 1), blk(T.g2, 4), bank(dbank[1, 1], 128), A.add, a_g[1, 1])))
+        v_qx.append(quant(1, add(3, 1, a_g3[1])))
 
     p_y = [mm(bank(7 * h, 128), T.vq[:], T.vp[:], blk(T.xq, h), blk(T.xp, h), v_qv, v_qx[h]) for h in range(2)]
     y = [act(T.ys[:, 0:128], bank(0, 128), AF.Copy, None, None, p_y[0]), cp(T.ys[:, 128:256], bank(7, 128), p_y[1])]
     for h in range(2):
         dma("s", "dout", blk(T.oc, h, 512), blk(T.xq, h).bitcast(dt.uint8), v_qx[h])
+    for h in range(2):
         dma("s", "dout", blk(T.y, h), blk(T.ys, h), y[h])
     for k in range(4):
         end = dma("a", "dout", T.osc[4 * k:4 * k + 4, :], T.xp[32 * k:32 * k + 4, :], v_qx[1])

@@ -1,11 +1,10 @@
-from concourse.bass import DstId, RemoteDMATransfer
 from concourse.mybir import dt, AluOpType, ActivationFunctionType
 
 C, K, R = 256, 64, 3
 Z0 = 16
 PL = Z0 + C
+NV = 64
 X4, U8, F32, BF, I32, U16 = "float8_e4m3fn_x4", "uint8", "float32", "bfloat16", "int32", "uint16"
-LW = 128 + K * R
 
 
 def sb(n, d):
@@ -16,33 +15,35 @@ SCRATCH = {
     "xin": sb(1024, BF), "uin": sb(512, BF), "vin": sb(512, BF), "blrow": sb(128, I32),
     "wq": sb(512, X4), "wp": sb(512, U8), "uq": sb(128, X4), "up": sb(128, U8), "uq2": sb(128, X4), "up2": sb(128, U8),
     "vq": sb(128, X4), "vp": sb(128, U8), "eq": sb(512, X4), "ep": sb(512, U8),
-    "xq": sb(256, X4), "xp": sb(256, U8), "xn": sb(1024, BF),
-    "lq": sb(LW, X4), "lp": sb(LW, U8), "zt": sb(512, BF),
+    "xn": sb(1024, BF), "zq": sb(128, X4), "zp": sb(128, U8), "zt": sb(512, BF),
     "ebuf": sb(528, BF), "ones": sb(136, BF),
     "ppin": sb(128, F32), "pp": sb(128, F32), "io32": sb(16, F32), "off": sb(32, U16),
-    "tl": sb(128, BF), "lidx": sb(256, BF), "k0": sb(128, BF), "kj": sb(96, BF),
-    "c1": sb(128, BF), "c2": sb(256, BF), "g16": sb(64, BF), "j8": sb(128, F32), "w8": sb(128, BF),
+    "tl": sb(128, BF), "lidx": sb(256, BF), "diag": sb(128, BF), "k0": sb(96, BF), "kj": sb(96, BF),
+    "c1": sb(128, BF), "c2": sb(C + K, BF), "j8": sb(128, F32), "w8": sb(128, BF),
     "cols": sb(8, F32), "bt": sb(128, BF), "an": sb(128, BF),
     "d0": sb(512, BF), "st": sb(640, BF), "l0": sb(192, BF), "l1": sb(192, BF), "lim": sb(192, BF),
     "ww": sb(64, BF), "sg": sb(64, BF), "pi": sb(64, BF), "fs": sb(192, BF), "fd": sb(384, F32), "tab": sb(384, F32),
-    "mm": sb(256, F32), "dd": sb(256, BF), "gs": sb(256, BF), "ne": sb(64, BF), "se": sb(128, F32),
-    "oe": sb(8 * R, U16), "lb": sb(8 * R, U16), "lm": sb(4 * R + 4, F32), "up1": sb(32, F32), "dn1": sb(32, F32),
-    "lf": sb(8, F32), "bb": sb(16, F32), "of": sb(8, F32), "ob1": sb(16, F32), "ob2": sb(8, F32),
-    "t2": sb(4 * PL, BF), "tf": sb(512, BF), "nn": sb(256, BF),
-    "lc": sb(16, U16), "nf": sb(128, BF), "cs": sb(128, BF),
-    "ha": sb(264, F32), "hb": sb(264, F32), "g2": sb(640, F32),
+    "mm": sb(256, F32), "dd": sb(C + K, BF), "gs": sb(C + K, BF), "se": sb(128, F32),
+    "oe": sb(8 * R, U16), "lb": sb(8 * R, U16), "up1": sb(8, F32), "dn1": sb(8, F32),
+    "lf": sb(8, F32), "bb": sb(16, F32), "ob2": sb(8, F32),
+    "t2": sb(4 * PL, BF), "tf": sb(2 * C + NV, BF), "nn": sb(256, BF),
+    "lc": sb(16 * R, U16), "ld": sb(16 * R, U16), "nf": sb(128, BF), "cs": sb(128, BF),
+    "ha": sb(264, F32), "hb": sb(264, F32), "g2": sb(512, F32),
     "ys": sb(256, F32), "ps": ("psum", [128, 4096], F32),
 }
-for _t in range(1, R):
-    SCRATCH["zq%d" % _t] = sb(128, X4)
-    SCRATCH["zp%d" % _t] = sb(128, U8)
-SEMAPHORES = ["sv", "sa", "sp", "sg", "dbl", "du", "dx", "dw", "dv", "dout", "sent", "am"] + \
-    ["az%d" % t for t in range(R)] + ["ac%d" % t for t in range(R)]
+for _t in range(R + 1):
+    SCRATCH["xq%d" % _t] = sb(C, X4)
+    SCRATCH["xp%d" % _t] = sb(C, U8)
+for _t in range(R):
+    SCRATCH["rq%d" % _t] = sb(C, X4)
+    SCRATCH["rp%d" % _t] = sb(C, U8)
+SEMAPHORES = ["sv", "sa", "sp", "sg", "dbl", "du", "dx", "dx1", "dw", "dv", "dout", "sent"] + \
+    ["%s%d" % (s, t) for s in ("ax", "ay", "ac", "al") for t in range(R)]
 
 A = AluOpType
 AF = ActivationFunctionType
 BIG = 1e29
-SC = 16384.0
+SC = 32768.0
 
 
 def rank_program(g, core, T, topo):
@@ -136,23 +137,21 @@ def rank_program(g, core, T, topo):
 
     off = T.off
     peers = [T.cores[rank ^ (1 << t)] for t in range(R)]
-    for n in range(4):
-        k_bl = dma("sa"[n % 2], "dbl", T.blrow[32 * n + 31:32 * n + 32, :], T.bl[32 * n:32 * n + 32, :])
+    k_bl = dma("s", "dbl", T.blrow[0:128:32, :], T.bl[:], ms(T.blrow[:], 0))
     k_u = dma("s", "du", T.uin[:], T.u[:])
-    k_x = dma("s", "dx", T.xin[:], T.x[:])
+    k_x = dma("s", "dx", blk(T.xin, 0, 512), blk(T.x, 0, 512))
+    k_x1 = dma("s", "dx1", blk(T.xin, 1, 512), blk(T.x, 1, 512))
     dma("s", "dw", T.wq[:].bitcast(dt.uint8), T.wc[:], k_u)
     k_w = dma("s", "dw", T.wp[:], T.ws[:])
 
     m_e = ms(T.ebuf[:], 0.0)
     m_one = ms(T.ones[:], 1.0)
-    i_pp = iota(T.ppin[:, 0:32], [[0, 2], [1, 4], [16, 4]], 0)
+    i_e = done("g", g.iota(T.diag[:], [[-1, 128]], 0, 1, allow_small_or_imprecise_dtypes=True))
+    iota(T.ppin[:, 0:32], [[0, 2], [1, 4], [16, 4]], 0)
+    i_pp = iota(T.ppin[:, 32:64], [[0, 16], [-64, 2]], 32)
     i_bl = iota(T.io32[:, 0:8], [[4, 4], [64, 2]], 0)
-    wait("g", m_e)
-    i_e = done("g", g.affine_select(T.ebuf[:, 3:515:4], T.ebuf[:, 3:515:4], [[-1, 128]], A.not_equal, 1.0, 0, 1))
-    i_t0 = iota(T.tl[:, 0:32], [[1, 16], [0, 2]], 0)
-    i_lk = iota(T.ppin[:, 32:64], [[0, 16], [-64, 2]], 32)
-    i_tl = iota(T.tl[:, 32:128], [[0, 3], [1, 16], [0, 2]], 0)
-    iota(T.ppin[:, 64:96], [[0, 2], [1, 16]], 0)
+    i_tl = iota(T.tl[:], [[0, 4], [1, 16], [0, 2]], 0)
+    i_ln = iota(T.ppin[:, 64:96], [[0, 2], [1, 16]], 0)
     i_p2 = iota(T.ppin[:, 96:128], [[0, 4], [-2, 4], [7, 2]], 7)
     i_lx = iota(T.lidx[:], [[1, 16], [0, 16]], 0)
 
@@ -165,57 +164,71 @@ def rank_program(g, core, T, topo):
     fill(T.fd[:, 1:384:3], 128, 0.0)
     for b in range(4):
         fill(T.t2[:, PL * b:PL * b + Z0], Z0, 0.0)
-    for a in range(0, 128, 32):
-        ms(T.blrow[a:a + 31, :], 0)
-    v_pp = tr(T.pp[:, 0:32], T.ppin[:, 0:32], i_pp)
+    v_id = ts(T.ebuf[:, 3:515:4], T.diag[:], 0.0, A.is_equal, None, None, i_e, m_e)
     ms(T.zt[:, 256:512], 0.0)
 
     def unit(b):
-        return qz(blk(T.eq, b), blk(T.ep, b), T.ebuf[:, 3 - b:515 - b], i_e)
+        return qz(blk(T.eq, b), blk(T.ep, b), T.ebuf[:, 3 - b:515 - b], v_id)
 
-    v_e = [unit(0)]
+    v_e = [unit(0), unit(1)]
+    v_pp = tr(T.pp[:, 0:64], T.ppin[:, 0:64], i_pp)
+    v_e.append(unit(2))
     v_lb = ts(off[:, 0:8], T.io32[:, 0:8], T.pp[:, 0:1], A.add, None, None, v_pp, i_bl)
-    v_e.append(unit(1))
+    v_e.append(unit(3))
+    line = T.pp[:, 64:65]
 
     t32 = T.tl[:, 0:32]
-    a_lk = lin(T.io32[:, 8:16], T.tl[:, 0:8], 1.0, -1.5, i_t0)
-    a_ab = act(blk(T.k0, 3, 32), t32, AF.Abs, 1.0 / 64, -7.5 / 64)
+    a_lk = lin(T.io32[:, 8:16], T.tl[:, 0:8], 1.0, -1.5, i_tl)
+    a_ab = act(blk(T.k0, 0, 32), t32, AF.Abs, 1.0 / 64, -7.5 / 64)
     lin(T.st[:, 2:128:4], t32, 1.0 / 64, 48.0 / 64)
-    lin(blk(T.k0, 0, 32), t32, 1.0 / 64, 48.0 / 64)
     lin(blk(T.k0, 1, 32), t32, -1.0 / 64, -48.0 / 64)
-    a_k0 = lin(blk(T.k0, 2, 32), blk(T.k0, 3, 32), 1.0, -55.5 / 64, a_ab)
-    a_kj = lin(T.kj[:], T.tl[:, 32:128], 1.0 / 64, -63.0 / 64, i_tl)
+    a_k0 = lin(blk(T.k0, 2, 32), blk(T.k0, 0, 32), 1.0, -55.5 / 64, a_ab)
+    a_kj = lin(T.kj[:], T.tl[:, 32:128], 1.0 / 64, -63.0 / 64)
     lin(T.l1[:, 0:192:2], T.tl[:, 32:128], 1.0 / 64, 1.0 / 64)
 
+    v_lu = ts(off[:, 16:24], T.tl[:, 0:16:2], 16.0, A.mult, None, None, i_tl)
     v_bt = ts(T.bt[:], T.blrow[:].indirect(off[:, 0:8]), 1.0 / 64, A.mult, -63.0 / 64, A.add, k_bl, v_lb)
-    x = tr(T.pp[:, 32:64], T.ppin[:, 32:64], i_lk)
-    v_lu = ts(off[:, 16:24], T.tl[:, 0:16:2], 16.0, A.mult, None, None)
+    v_lk = ts(off[:, 8:16], T.io32[:, 8:16], T.pp[:, 32:33], A.mult, 48.0, A.add, a_lk)
+    v_ln = tr(T.pp[:, 64:96], T.ppin[:, 64:96], i_ln)
     v_an = tr(T.an[:], T.bt[:], v_bt)
-    v_lk = ts(off[:, 8:16], T.io32[:, 8:16], T.pp[:, 32:33], A.mult, 48.0 + 31, A.add, x, a_lk)
-    v_e.append(unit(2))
+    v_qu = qz(T.uq[:], T.up[:], T.uin[:], k_u)
     k_0, k_1 = T.an[:].indirect(off[:, 8:10]), T.an[:].indirect(off[:, 10:16])
-    a_mf = lin(blk(T.lm, R, 4), T.an[:, 31:128:32], 64.0, 62.0, v_an)
-    act(T.d0[:, 1:128:4], k_0, AF.Copy, None, None, v_lk)
+    act(T.d0[:, 1:128:4], k_0, AF.Copy, None, None, v_an, v_lk)
     a_n0 = lin(T.d0[:, 3:128:4], k_0, -1.0, -63.0 / 64)
     a_th = act(T.l1[:, 1:192:2], k_1, AF.Copy, -1.0, None)
     act(T.d0[:, 129:512:4], k_1, AF.Copy, None, None)
     a_n1 = lin(T.d0[:, 131:512:4], T.l1[:, 1:192:2], 1.0, -63.0 / 64, a_th)
+    a_pu = act(T.up2[:], T.up[:].indirect(off[:, 16:24]), AF.Copy, None, None, v_qu, v_lu)
+    for h in range(2):
+        lin(T.fd[:, 192 * h + 2:192 * h + 192:3], T.tl[:, 0:128:2], -1.0 / 64 - 1.0 / SC, 2.0 + 15.0 / SC)
+    fill(T.dd[:, 127:128], 1, 0.0)
+    fill(T.dd[:, 255:C + K], K + 1, 0.0)
+    x = fill(T.c2[:, C:C + K], K, 1.0 / 64)
+    fill(T.c2[:, C + 16:C + K:16], 3, -15.0 / 64, x)
+    fill(T.c2[:, C:C + 1], 1, 0.0)
 
-    allowed = [topo.engines(core, p) for p in peers]
-    narrow = min(allowed, key=len)
-    far = [t for t in range(R) if len(allowed[t]) == len(narrow)]
-    near = [t for t in range(R) if t not in far]
-    share = {}
-    for n, t in enumerate(far):
-        share[t] = narrow[n * len(narrow) // len(far):(n + 1) * len(narrow) // len(far)]
-    for t in near:
-        share[t] = [e for e in allowed[t] if e not in narrow]
-    wait("g", a_mf)
-    g.remote_dma_fused([RemoteDMATransfer(dst_ids=[DstId(rid=topo.addr(peers[t])[0], pnc=topo.addr(peers[t])[1])],
-                                          dma_engine_mask=bits(share[t]), remote_sem=T.sem.am,
-                                          src=blk(T.lm, R, 4), dst=blk(T.lm, t, 4)) for t in range(R)], local_sem=T.sem.sent)
-    sent = [sum(len(share[t]) for t in range(R))]
-    k_m = ("am", sent[0])
+    sent = [0]
+
+    def send(t, dst, src, sem, *d):
+        rid, pid, _se = topo.addr(peers[t])
+        eng = topo.engines(core, peers[t])
+        wait("g", *d)
+        g.remote_dma(dst, src, T.sem["%s%d" % (sem, t)], T.sem.sent, pid, rid, bits(eng))
+        sent[0] += len(eng)
+
+    def landed(t, sem, n=1):
+        return ("%s%d" % (sem, t), n * len(topo.engines(peers[t], core)))
+
+    def codes(name, t, h):
+        return blk(T["%sq%d" % (name, t)], h), blk(T["%sp%d" % (name, t)], h)
+
+    def quant(t, h, src, *d):
+        return qz(*codes("x", t, h), blk(src, h, 512), *d)
+
+    def send_x(t, qx):
+        send(t, codes("r", t, 0)[0].bitcast(dt.uint8), codes("x", t, 0)[0].bitcast(dt.uint8), "ax", qx[0])
+        send(t, T["rp%d" % t][:], T["xp%d" % t][:], "ax", qx[1])
+        send(t, codes("r", t, 1)[0].bitcast(dt.uint8), codes("x", t, 1)[0].bitcast(dt.uint8), "ay")
 
     def sl(buf, s, a):
         return buf[:, 128 * s + a:128 * s + 128:4]
@@ -237,12 +250,12 @@ def rank_program(g, core, T, topo):
     def right(buf, a):
         return buf[:, a + 508:a + 3:-8]
 
-    def products(qx, *d):
-        s = [mm(bank(7 * h, 128), T.uq2[:], T.up2[:], blk(T.xq, h), blk(T.xp, h), qx[h], *d) for h in range(2)]
-        return s, [mm(bank(1 + b, C), blk(T.eq, b), blk(T.ep, b), T.xq[:], T.xp[:], v_e[b]) for b in range(4)]
+    def products(t, qx, *d):
+        s = [mm(bank(7 * h, 128), T.uq2[:], T.up2[:], *codes("x", t, h), qx[h], *d) for h in range(2)]
+        return s, [mm(bank(1 + b, C), blk(T.eq, b), blk(T.ep, b), T["xq%d" % t][:], T["xp%d" % t][:], v_e[b]) for b in range(4)]
 
-    def half_t(b, p):
-        return act(T.t2[:, PL * b + Z0:PL * b + PL], bank(1 + b, C), AF.Copy, 0.5, None, p[b])
+    def keep_t(p):
+        return [act(T.tf[:, C * b:C * b + n], bank(1 + b, n), AF.Copy, None, None, p[b]) for b, n in enumerate((C, C, NV))]
 
     def gap_min(h, *d):
         return scan(blk(T.mm, h), T.c1[:], bank(7 * h, 128), 0.0, A.add, A.min, *d)
@@ -253,172 +266,149 @@ def rank_program(g, core, T, topo):
     def gap_last(*d):
         return scan(T.gs[:], T.c2[:], T.dd[:], 1.0, A.add, A.max, *d)
 
-    gp = T.gs[:, 255:256]
+    def gap_mark(*d):
+        return lin(T.cols[:, 6:7], T.gs[:, 255:256], 0.5, 1.0, *d)
 
-    def gap_mask(*d):
-        return ts(T.ne[:], T.g16[:], gp, A.not_equal, None, None, *d)
+    gp = T.cols[:, 6:7]
 
     tt(sl(T.st, 0, 0), k_0, blk(T.k0, 1, 32), A.is_gt, v_an, v_lk, a_k0)
-    tt(sl(T.st, 0, 1), k_0, blk(T.k0, 0, 32), A.add)
-    x = tt(sl(T.d0, 0, 2), k_0, blk(T.k0, 2, 32), A.is_le)
+    tt(sl(T.d0, 0, 2), k_0, blk(T.k0, 2, 32), A.is_le)
+    x = tt(sl(T.st, 0, 1), k_0, sl(T.st, 0, 2), A.add)
     y = tt(T.l0[:, 1:192:2], k_1, T.kj[:], A.is_le, a_kj)
     x = place(0, x, a_n0)
-    v_qu = qz(T.uq[:], T.up[:], T.uin[:], k_u)
+    v_qx = [quant(0, 0, T.xin, k_x)]
     v_lim = scan(T.lim[:], T.l0[:], T.l1[:], 0.0, A.mult, A.add, y, a_th)
     x = tests(1, x)
-    a_pu = act(T.up2[:], T.up[:].indirect(off[:, 16:24]), AF.Copy, None, None, v_qu, v_lu)
     v_pu = cp(T.uq2[:].bitcast(dt.uint32), T.uq[:].bitcast(dt.uint32).indirect(off[:, 16:24]), v_qu, v_lu)
     x = place(1, x, a_n1)
-    v_p2 = tr(T.pp[:, 64:128], T.ppin[:, 64:128], i_p2)
-    v_e.append(unit(3))
-    line = T.pp[:, 64:65]
-    lin(T.cols[:, 0:1], line, 16.0 / SC, (Z0 - 64.0) / SC, v_p2)
+    v_qx.append(quant(0, 1, T.xin, k_x1))
+    send_x(0, v_qx)
+    p_s, p_d = products(0, v_qx, v_pu, a_pu)
+    lin(T.cols[:, 0:1], line, 16.0 / SC, (Z0 - 64.0) / SC)
     lin(T.cols[:, 1:2], line, 16.0 / SC, (Z0 + 64.0) / SC)
     lin(T.cols[:, 2:3], line, 2.0, 1.0)
-    a_cols = lin(T.cols[:, 3:4], line, 16.0, float(Z0))
-    for h in range(2):
-        lin(T.fd[:, 192 * h + 2:192 * h + 192:3], T.tl[:, 0:128:2], -1.0 / 32 - 1.0 / SC, 2.0 + 15.0 / SC)
-    fill(T.dd[:, 127:256:128], 2, 0.0)
-    a_g16 = lin(T.g16[:], T.tl[:, 0:128:2], -1.0 / 32, 2.0)
+    for n, c in ((3, 0.0), (4, 15.0), (5, 16.0)):
+        a_cols = lin(T.cols[:, n:n + 1], line, 16.0, Z0 + c)
+    for k in range(4):
+        fill(T.w8[:, 2 * k + 1:128:8], 16, 96.0 - 32 * k)
+    fill(T.up1[:, 0:8:2], 4, 1000.0)
+    fill(T.dn1[:, 0:8:2], 4, -1000.0)
+    lin(T.up1[:, 1:8:2], T.an[:, 0:128:32], 64.0, 62.0)
+    lin(T.dn1[:, 1:8:2], T.an[:, 96::-32], -64.0, -62.0)
     x = tests(2, x)
-    v_qx = [qz(blk(T.xq, 0), blk(T.xp, 0), blk(T.xin, 0, 512), k_x)]
-    x = place(2, x)
-    v_qx.append(qz(blk(T.xq, 1), blk(T.xp, 1), blk(T.xin, 1, 512)))
-    p_s, p_d = products(v_qx, v_pu, a_pu)
-    x = tests(3, x)
-    c2 = ts(T.c2[:], T.lidx[:], line, A.is_equal, -1.0 / 32, A.mult, i_lx, v_p2)
-    c2 = act(T.c2[:, 15:256:16], T.c2[:, 0:256:16], AF.Copy, -32.0, None, c2)
-    x3 = place(3, x)
     z0 = gap_min(0, p_s[0])
+    x = place(2, x)
+    c2 = ts(T.c2[:, 0:C], T.lidx[:], line, A.is_equal, -1.0 / 32, A.mult, i_lx)
+    c2 = act(T.c2[:, 15:256:16], T.c2[:, 0:256:16], AF.Copy, -32.0, None, c2)
+    x = tests(3, x)
+    z1 = gap_min(1, p_s[1])
+    x3 = place(3, x)
+    gap_less(0, z0)
     a_vh = lin(T.fd[:, 0:192:3], right(T.st, 131), -64.0 / SC, T.cols[:, 1:2], x3, a_cols)
     a_ve = lin(T.fd[:, 192:384:3], left(T.st, 131), 64.0 / SC, T.cols[:, 0:1])
-    a_t2 = [half_t(b, p_d) for b in range(4)]
+    a_tf = keep_t(p_d)
     v_ww = tt(T.ww[:], left(T.d0, 2), right(T.d0, 2), A.add, x)
     y = scan(T.pi[:], left(T.st, 131), right(T.st, 131), 4.0, A.min, A.add, x3)
     x = scan(T.sg[:], left(T.st, 130), right(T.st, 130), 4.0, A.min, A.add)
-    z1 = gap_min(1, p_s[1])
+    z = gap_less(1, z1)
     tt(T.fs[:, 2:192:3], T.pi[:], T.ww[:], A.is_le, y, v_ww)
     x = ts(T.fs[:, 1:192:3], T.sg[:], 130.0 / 64, A.is_ge, None, None, x)
-    gap_less(0, z0)
-    z = gap_less(1, z1)
-    v_tab = scan(blk(T.tab, 0, 192), T.fs[:], blk(T.fd, 0, 192), 0.0, A.mult, A.add, x, a_vh)
     v_gp = gap_last(z, c2)
+    v_tab = scan(blk(T.tab, 0, 192), T.fs[:], blk(T.fd, 0, 192), 0.0, A.mult, A.add, x, a_vh)
     v_tae = scan(blk(T.tab, 1, 192), T.fs[:], blk(T.fd, 1, 192), 0.0, A.mult, A.add, a_ve)
-    v_ne = gap_mask(v_gp, a_g16)
-    cp(off[:, 24:32], T.pp[:, 96:104])
-
-    def covered(lists, n, tmp, out, *d):
-        ts(tmp[:, 0:8:2], lists[0], T.cols[:, 3:4], A.subtract, None, None, *d)
-        x = ts(tmp[:, 1:8:2], lists[1], T.cols[:, 3:4], A.subtract, None, None)
-        scan(out[:, 0:8], blk(T.up1, n, 8), tmp[:, 0:8], 0.0, A.add, A.min, x, a_m)
-        return scan(out[:, 15:7:-1], blk(T.dn1, R - n, 8), tmp[:, 7::-1], 0.0, A.add, A.max)
+    a_gp = gap_mark(v_gp)
+    for h in range(2):
+        lin(T.j8[:, h:128:2], T.lidx[:, 0:256:4], -1.0, T.cols[:, 4 + h:5 + h])
+    a_w8 = lin(T.w8[:, 0:128:2], T.w8[:, 1:128:2], 1.0, T.cols[:, 2:3])
+    v_p2 = tr(T.pp[:, 96:128], T.ppin[:, 96:128], i_p2)
 
     v_qv = None
     for t in range(R):
         last = t == R - 1
-        rid, pid, _se = topo.addr(peers[t])
-        eng = allowed[t]
-        mask = bits(eng)
-        lo = 128 + K * t
-        oe = blk(T.oe, t, 8)
         if t > 0:
-            a_t2 = [half_t(b, p_d) for b in range(4)]
+            a_tf = keep_t(p_d)
             z = [gap_min(h, p_s[h]) for h in range(2)]
-            v_ne = gap_mask(gap_last([gap_less(h, z[h]) for h in range(2)][1]))
-        x = scan(T.se[:, K:2 * K], T.ne[:], T.tab[:, 2:192:3], 4.0, A.mult, A.max, v_ne, v_tab)
-        y = scan(T.se[:, 0:K], T.ne[:], T.tab[:, 194:384:3], 4.0, A.mult, A.max, v_tae)
-        e_list, h_list = T.oe[:, 8 * t:8 * t + 4], T.oe[:, 8 * t + 4:8 * t + 8]
-        v_off = ts(h_list, T.se[:, K + 15:2 * K:16], gp, A.subtract, SC, A.mult, x)
-        v_ofe = ts(e_list, T.se[:, 15:K:16], gp, A.subtract, SC, A.mult, y)
-        wait("g", v_ofe)
-        g.remote_dma(blk(T.lb, t, 8), oe, T.sem["ac%d" % t], T.sem.sent, pid, rid, mask)
+            v_gp = gap_last([gap_less(h, z[h]) for h in range(2)][1])
+            a_gp = gap_mark(v_gp)
+        scan(T.se[:, K:2 * K], T.gs[:, C:C + K], T.tab[:, 2:192:3], 0.0, A.min, A.max, v_gp, v_tab)
+        x = scan(T.se[:, 0:K], T.gs[:, C:C + K], T.tab[:, 194:384:3], 0.0, A.min, A.max, v_tae)
+        if t == 0:
+            cp(off[:, 24:32], T.pp[:, 96:104], v_p2)
+        send(t, blk(T.lb, t, 8), blk(T.oe, t, 8), "ac", ts(blk(T.oe, t, 8), T.se[:, 15:128:16], gp, A.subtract, SC, A.mult, x, a_gp))
+        a_t2 = {}
+        for h, banks in enumerate(((5, 6, 1, 2), (0, 7, 5, 6))):
+            free = [v_gp, v_gp, a_t2[0, 0], a_t2[1, 0]] if h else [p_d[0], p_d[0]] + a_tf[:2]
+            for b in range(4):
+                p = mm(bank(banks[b], 128), blk(T.eq, b), blk(T.ep, b), *codes("r", t, h),
+                       landed(t, "ay") if h else landed(t, "ax", 2), free[b])
+                a = PL * b + Z0 + 128 * h
+                a_t2[b, h] = act(T.t2[:, a:a + 128], bank(banks[b], 128), AF.Copy, 0.5, None, p)
+        ts(T.lf[:, 0:8:2], T.se[:, 15:K:16], gp, A.subtract, SC, A.mult)
+        x = ts(T.lf[:, 1:8:2], T.se[:, K + 15:2 * K:16], gp, A.subtract, SC, A.mult)
+        if t == 0:
+            ms(T.ha[:, 0:258:2], 0.0)
+        scan(T.bb[:, 0:8], T.up1[:], T.lf[:], 0.0, A.add, A.min, x, a_w8)
+        x = scan(T.bb[:, 15:7:-1], T.dn1[:], T.lf[:, 7::-1], 0.0, A.add, A.max)
+        if t == 0:
+            ms(T.hb[:, 0:258:2], 0.0)
+        x = tt(T.nf[:], T.bb[:].indirect(off[:, 24:32]), T.j8[:], A.is_lt, x)
+        if last:
+            ts(T.ob2[:, 0:8:2], T.bb[:, 8:16:2], T.cols[:, 3:4], A.subtract, -1.0, A.max)
+            dma("s", "dout", T.ob[:], T.ob2[:], ts(T.ob2[:, 1:8:2], T.bb[:, 1:8:2], T.cols[:, 3:4], A.subtract, -1.0, A.max))
+        v_cs = scan(T.cs[:], T.nf[:], T.w8[:], 128.0, A.mult, A.max, x)
 
         def win(b):
             return blk(T.t2, b, PL)
 
-        a_n = [None] + [act(blk(T.nn, b, K), win(b).indirect(h_list), AF.Copy, None, None, v_off, a_t2[b])
+        e_list, h_list = T.lb[:, 8 * t:8 * t + 4], T.lb[:, 8 * t + 4:8 * t + 8]
+        k_c, k_l = landed(t, "ac"), landed(t, "al")
+        a_n = [None] + [act(blk(T.nn, b, K), win(b).indirect(h_list), AF.Copy, None, None, k_c, a_t2[b, 1])
                         for b in range(1, 4)]
-        a_n[0] = cp(T.nn[:, 0:K], win(0).indirect(h_list), v_off, a_t2[0])
+        a_n[0] = cp(T.nn[:, 0:K], win(0).indirect(h_list), k_c, a_t2[0, 1])
+        send(t, blk(T.ld, t, 16), blk(T.lc, t, 16), "al", cp(blk(T.lc, t, 16), T.cs[:, 127:6:-8], v_cs))
         for b in range(4):
-            x = tt(T.zt[:, b:256:4], win(b).indirect(e_list), blk(T.nn, b, K), A.add, a_n[b], v_ofe)
-        zq, zp = (T["zq%d" % t], T["zp%d" % t]) if t else (T.lq, T.lp)
-        v_qz = qz(zq[:, 0:128], zp[:, 0:128], T.zt[:], x)
-        wait("g", v_qz)
-        g.remote_dma(T.lq[:, lo:lo + K].bitcast(dt.uint8), zq[:, 0:K].bitcast(dt.uint8), T.sem["az%d" % t], T.sem.sent, pid, rid, mask)
-        g.remote_dma(T.lp[:, lo:lo + K], zp[:, 0:K], T.sem["az%d" % t], T.sem.sent, pid, rid, mask)
-        sent[0] += 3 * len(eng)
-        if t == 0:
-            x = [fill(T.w8[:, 2 * k + 1:128:8], 16, 96.0 - 32 * k) for k in range(4)][3]
-            fill(T.up1[:, 0:32:2], 16, 1000.0)
-            fill(T.dn1[:, 0:32:2], 16, -1000.0)
-            act(T.up1[:, 1:32:2], T.lm[:], AF.Copy, None, None, k_m)
-            a_m = act(T.dn1[:, 1:32:2], T.lm[:, 15::-1], AF.Copy, -1.0, None)
-            for h in range(2):
-                lin(T.j8[:, h:128:2], T.lidx[:, 0:256:4], -1.0, 15.0 + h)
-            a_w8 = lin(T.w8[:, 0:128:2], T.w8[:, 1:128:2], 1.0, T.cols[:, 2:3], x)
-            fill(T.ha[:, 0:258:2], 129, 0.0)
-            a_hz = fill(T.hb[:, 0:258:2], 129, 0.0)
-        a_tf = [act(blk(T.tf, b, C), bank(1 + b, C), AF.Copy, None, None) for b in range(2)]
+            x = tt(T.zt[:, b:256:4], win(b).indirect(e_list), blk(T.nn, b, K), A.add, a_n[b])
         if t == 1:
             v_qv = qz(T.vq[:], T.vp[:], T.vin[:], k_v)
-        if last:
-            x = covered((e_list, h_list), R, T.of, T.ob1)
-            ts(T.ob2[:, 0:8:2], T.ob1[:, 8:16:2], -1.0, A.max, None, None, x)
-            x = ts(T.ob2[:, 1:8:2], T.ob1[:, 1:8:2], -1.0, A.max, None, None)
-            dma("s", "dout", T.ob[:], T.ob2[:], x)
-        x = covered((blk(T.lb, 2 * t, 4), blk(T.lb, 2 * t + 1, 4)), t, T.lf, T.bb, ("ac%d" % t, len(eng)))
-        x = tt(T.nf[:], T.bb[:].indirect(off[:, 24:32]), T.j8[:], A.is_lt, x, a_w8)
-        x = scan(T.cs[:], T.nf[:], T.w8[:], 128.0, A.mult, A.max, x)
-        v_lc = cp(T.lc[:], T.cs[:, 127:6:-8], x)
-        hk = {0: 0, 2: 7, 1: 5, 3: 6}
-        p_h = {b: mm(bank(hk[b], 128), blk(T.wq, b), blk(T.wp, b), T.lq[:, lo - K:lo + K], T.lp[:, lo - K:lo + K],
-                     k_w, v_qz, ("az%d" % t, 2 * len(eng))) for b in hk}
+        v_qz = qz(T.zq[:], T.zp[:], T.zt[:], x)
+        hk = {0: 1, 3: 7, 2: 2, 1: 0}
+        p_h = {b: mm(bank(hk[b], 128), blk(T.wq, b), blk(T.wp, b), T.zq[:], T.zp[:], k_w, v_qz) for b in hk}
 
         def h_out(b):
             return (T.ha, T.hb)[b // 2][:, 128 * (b % 2) + 1:128 * (b % 2) + 128:2]
 
-        def h_pick(b, a, n):
-            return (T.ha, T.hb)[b // 2][:, 128 * (b % 2):128 * (b % 2) + 129].indirect(T.lc[:, a:a + n])
+        def h_pick(b, a, z):
+            return (T.ha, T.hb)[b // 2][:, 128 * (b % 2):128 * (b % 2) + 129].indirect(
+                T.ld[:, 16 * t + a // 16:16 * t + z // 16])
 
-        def new(b, h, n=1):
-            return T.xn[:, 512 * h + b:512 * (h + n):4]
-
-        def quant(h, *d):
-            return qz(blk(T.xq, h), blk(T.xp, h), blk(T.xn, h, 512), *d)
-
-        def add(b, h, *d):
-            return tt(new(b, h), blk(T.g2, 2 * b - 4 + h), bank(1 + b, 128 * h + 128, 128 * h), A.add, *d)
+        def new(b, a, z):
+            return T.xn[:, 4 * a + b:4 * z:4]
 
         if t == 0:
             k_v = dma("s", "dv", T.vin[:], T.v[:], p_h[2])
-        v_h0 = ts(h_out(0), bank(hk[0], 128, K), 0.03125, A.mult, None, None, p_h[0], a_hz)
-        a_h2 = act(h_out(2), bank(hk[2], 128, K), AF.Copy, 0.03125, None, p_h[2])
-        a_h1 = act(h_out(1), bank(hk[1], 128, K), AF.Copy, 0.03125, None, p_h[1])
-        a_g2 = act(blk(T.g2, 0, C), h_pick(2, 0, 16), AF.Copy, None, None, a_h2, v_lc)
-        tt(new(0, 0, 2), h_pick(0, 0, 16), blk(T.tf, 0, C), A.add, v_h0, v_lc, a_tf[0])
-        v_h3 = ts(h_out(3), bank(hk[3], 128, K), 0.03125, A.mult, None, None, p_h[3])
-        tt(new(1, 0, 2), h_pick(1, 0, 16), blk(T.tf, 1, C), A.add, a_h1, a_tf[1])
+        v_h0 = ts(h_out(0), bank(hk[0], K), 0.03125, A.mult, None, None, p_h[0])
+        v_h3 = ts(h_out(3), bank(hk[3], K), 0.03125, A.mult, None, None, p_h[3])
+        a_h2 = act(h_out(2), bank(hk[2], K), AF.Copy, 0.03125, None, p_h[2])
+        a_h1 = act(h_out(1), bank(hk[1], K), AF.Copy, 0.03125, None, p_h[1])
+        a_g3 = act(blk(T.g2, 1, C), h_pick(3, 0, C), AF.Copy, None, None, v_h3, k_l)
+        a_g2 = act(T.g2[:, NV:C], h_pick(2, NV, C), AF.Copy, None, None, a_h2)
+        tt(new(0, 0, C), h_pick(0, 0, C), blk(T.tf, 0, C), A.add, v_h0, k_l)
+        tt(new(1, 0, C), h_pick(1, 0, C), blk(T.tf, 1, C), A.add, a_h1)
+        tt(new(3, 0, C), blk(T.g2, 1, C), bank(4, C), A.add, a_g3)
+        tt(new(2, 0, NV), h_pick(2, 0, NV), T.tf[:, 2 * C:2 * C + NV], A.add)
+        x = [tt(new(2, a, z), T.g2[:, a:z], bank(3, z, a), A.add, a_g2) for a, z in ((NV, 128), (128, C))]
+        v_qx = [quant(t + 1, h, T.xn, x[h]) for h in range(2)]
         if not last:
-            a_g3 = act(blk(T.g2, 1, C), h_pick(3, 0, 16), AF.Copy, None, None, v_h3)
-            tt(new(2, 0, 2), blk(T.g2, 0, C), bank(3, C), A.add, a_g2)
-            x = [add(3, h, a_g3) for h in range(2)]
-            v_qx = [quant(h, x[h]) for h in range(2)]
-            p_s, p_d = products(v_qx)
-            continue
-        a_g3 = [act(blk(T.g2, 2 + h), h_pick(3, 8 * h, 8), AF.Copy, None, None, v_h3) for h in range(2)]
-        add(2, 0, a_g2)
-        x = add(3, 0, a_g3[0])
-        add(2, 1)
-        v_qx = [quant(0, x)]
-        v_qx.append(quant(1, add(3, 1, a_g3[1])))
+            send_x(t + 1, v_qx)
+            p_s, p_d = products(t + 1, v_qx)
 
-    p_y = [mm(bank(7 * h, 128), T.vq[:], T.vp[:], blk(T.xq, h), blk(T.xp, h), v_qv, v_qx[h]) for h in range(2)]
-    y = [act(T.ys[:, 0:128], bank(0, 128), AF.Copy, None, None, p_y[0]), cp(T.ys[:, 128:256], bank(7, 128), p_y[1])]
+    p_y = [mm(bank(7 * h, 128), T.vq[:], T.vp[:], *codes("x", R, h), v_qv, v_qx[h]) for h in range(2)]
+    y = [cp(blk(T.ys, h), bank(7 * h, 128), p_y[h]) for h in range(2)]
     for h in range(2):
-        dma("s", "dout", blk(T.oc, h, 512), blk(T.xq, h).bitcast(dt.uint8), v_qx[h])
+        dma("s", "dout", blk(T.oc, h, 512), codes("x", R, h)[0].bitcast(dt.uint8), v_qx[h])
     for h in range(2):
         dma("s", "dout", blk(T.y, h), blk(T.ys, h), y[h])
     for k in range(4):
-        end = dma("a", "dout", T.osc[4 * k:4 * k + 4, :], T.xp[32 * k:32 * k + 4, :], v_qx[1])
+        end = dma("a", "dout", T.osc[4 * k:4 * k + 4, :], T["xp%d" % R][32 * k:32 * k + 4, :], v_qx[1])
     wait("g", ("sent", sent[0]), ("sg", cnt["g"]), ("sp", cnt["p"]), ("sv", cnt["v"]), ("sa", cnt["a"]))
     wait("s", end)

from concourse.mybir import dt, AluOpType, ActivationFunctionType

C, K, R = 256, 64, 3
Z0 = 16
PL = Z0 + C
NV = 64
X4, U8, F32, BF, I32, U16 = "float8_e4m3fn_x4", "uint8", "float32", "bfloat16", "int32", "uint16"


def sb(n, d):
    return ("sbuf", [128, n], d)


SCRATCH = {
    "xin": sb(1024, BF), "uin": sb(512, BF), "vin": sb(512, BF), "blrow": sb(128, I32),
    "wq": sb(512, X4), "wp": sb(512, U8), "uq": sb(128, X4), "up": sb(128, U8), "uq2": sb(128, X4), "up2": sb(128, U8),
    "vq": sb(128, X4), "vp": sb(128, U8), "eq": sb(512, X4), "ep": sb(512, U8),
    "xn": sb(1024, BF), "zq": sb(128, X4), "zp": sb(128, U8), "zt": sb(512, BF),
    "ebuf": sb(528, BF), "ones": sb(136, BF),
    "ppin": sb(128, F32), "pp": sb(128, F32), "io32": sb(16, F32), "off": sb(32, U16),
    "tl": sb(128, BF), "lidx": sb(256, BF), "diag": sb(128, BF), "k0": sb(96, BF), "kj": sb(96, BF),
    "c1": sb(128, BF), "c2": sb(C + K, BF), "j8": sb(128, F32), "w8": sb(128, BF),
    "cols": sb(8, F32), "bt": sb(128, BF), "an": sb(128, BF),
    "d0": sb(512, BF), "st": sb(640, BF), "l0": sb(192, BF), "l1": sb(192, BF), "lim": sb(192, BF),
    "ww": sb(64, BF), "sg": sb(64, BF), "pi": sb(64, BF), "fs": sb(192, BF), "fd": sb(384, F32), "tab": sb(384, F32),
    "mm": sb(256, F32), "dd": sb(C + K, BF), "gs": sb(C + K, BF), "se": sb(128, F32),
    "oe": sb(8 * R, U16), "lb": sb(8 * R, U16), "up1": sb(8, F32), "dn1": sb(8, F32),
    "lf": sb(8, F32), "bb": sb(16, F32), "ob2": sb(8, F32),
    "t2": sb(4 * PL, BF), "tf": sb(2 * C + NV, BF), "nn": sb(256, BF),
    "lc": sb(16 * R, U16), "ld": sb(16 * R, U16), "nf": sb(128, BF), "cs": sb(128, BF),
    "ha": sb(264, F32), "hb": sb(264, F32), "g2": sb(512, F32),
    "ys": sb(256, F32), "ps": ("psum", [128, 4096], F32),
}
for _t in range(R + 1):
    SCRATCH["xq%d" % _t] = sb(C, X4)
    SCRATCH["xp%d" % _t] = sb(C, U8)
for _t in range(R):
    SCRATCH["rq%d" % _t] = sb(C, X4)
    SCRATCH["rp%d" % _t] = sb(C, U8)
SEMAPHORES = ["sv", "sa", "sp", "sg", "dbl", "du", "dx", "dx1", "dw", "dv", "dout", "sent"] + \
    ["%s%d" % (s, t) for s in ("ax", "ay", "ac", "al") for t in range(R)]

A = AluOpType
AF = ActivationFunctionType
BIG = 1e29
SC = 32768.0


def rank_program(g, core, T, topo):
    rank = T.rank_of(core)
    if rank is None:
        return
    Q = {"v": g.vector, "a": g.scalar, "p": g.tensor, "g": g, "s": g.sync}
    cnt = {"v": 0, "a": 0, "p": 0, "g": 0}
    seen = {q: {} for q in Q}

    def wait(q, *toks):
        for s, n in toks:
            if seen[q].get(s, 0) < n:
                Q[q].wait_ge(T.sem[s], n)
                seen[q][s] = n

    def done(q, ins):
        cnt[q] += 1
        ins.then_inc(T.sem["s" + q], 1)
        return ("s" + q, cnt[q])

    V = g.vector

    def ms(ap, c, *d):
        wait("v", *d)
        return done("v", V.memset(ap, c))

    def cp(o, i, *d):
        wait("v", *d)
        return done("v", V.tensor_copy(o, i))

    def tr(o, i, *d):
        wait("v", *d)
        return done("v", V.transpose(o, i))

    def tt(o, a, b, op, *d):
        wait("v", *d)
        return done("v", V.tensor_tensor(o, a, b, op))

    def ts(o, a, s1, op0, s2, op1, *d):
        wait("v", *d)
        if op1 is None:
            return done("v", V.tensor_scalar(o, a, s1, None, op0))
        return done("v", V.tensor_scalar(o, a, s1, s2, op0, op1))

    def scan(o, a, b, ini, op0, op1, *d):
        wait("v", *d)
        return done("v", V.tensor_tensor_scan(o, a, b, ini, op0, op1))

    def qz(o, s, i, *d):
        wait("v", *d)
        return done("v", V.quantize_mx(o, s, i))

    def act(o, i, f, scale, bias, *d):
        wait("a", *d)
        if bias is None and scale is None:
            return done("a", g.scalar.activation(o, i, f))
        if bias is None:
            return done("a", g.scalar.activation(o, i, f, scale=scale))
        return done("a", g.scalar.activation(o, i, f, bias=bias, scale=scale))

    def lin(o, i, scale, bias, *d):
        return act(o, i, AF.Identity, scale, bias, *d)

    def fill(o, n, c, *d):
        return act(o, T.ones[:, 0:n], AF.Copy, c, None, *d)

    def mm(o, w, ws, x, xs, *d):
        wait("p", *d)
        return done("p", g.tensor.matmul_mx(o, w, ws, x, xs, True, True))

    def iota(o, pat, base):
        return done("g", g.iota(o, pat, base, 0, allow_small_or_imprecise_dtypes=True))

    dn = {}

    def dma(q, s, o, i, *d):
        wait(q, *d)
        Q[q].dma_start(o, i).then_inc(T.sem[s], 16)
        dn[s] = dn.get(s, 0) + 16
        return (s, dn[s])

    def bank(b, n, a=0):
        return T.ps[:, 512 * b + a:512 * b + n]

    def blk(buf, b, n=128):
        return buf[:, n * b:n * b + n]

    def bits(engines):
        return sum(1 << e for e in engines)

    off = T.off
    peers = [T.cores[rank ^ (1 << t)] for t in range(R)]
    k_bl = dma("s", "dbl", T.blrow[0:128:32, :], T.bl[:], ms(T.blrow[:], 0))
    k_u = dma("s", "du", T.uin[:], T.u[:])
    k_x = dma("s", "dx", blk(T.xin, 0, 512), blk(T.x, 0, 512))
    k_x1 = dma("s", "dx1", blk(T.xin, 1, 512), blk(T.x, 1, 512))
    dma("s", "dw", T.wq[:].bitcast(dt.uint8), T.wc[:], k_u)
    k_w = dma("s", "dw", T.wp[:], T.ws[:])

    m_e = ms(T.ebuf[:], 0.0)
    m_one = ms(T.ones[:], 1.0)
    i_e = done("g", g.iota(T.diag[:], [[-1, 128]], 0, 1, allow_small_or_imprecise_dtypes=True))
    iota(T.ppin[:, 0:32], [[0, 2], [1, 4], [16, 4]], 0)
    i_pp = iota(T.ppin[:, 32:64], [[0, 16], [-64, 2]], 32)
    i_bl = iota(T.io32[:, 0:8], [[4, 4], [64, 2]], 0)
    i_tl = iota(T.tl[:], [[0, 4], [1, 16], [0, 2]], 0)
    i_ln = iota(T.ppin[:, 64:96], [[0, 2], [1, 16]], 0)
    i_p2 = iota(T.ppin[:, 96:128], [[0, 4], [-2, 4], [7, 2]], 7)
    i_lx = iota(T.lidx[:], [[1, 16], [0, 16]], 0)

    a_c1 = fill(T.c1[:], 128, 0.0, m_one)
    fill(T.d0[:, 0:512:4], 128, -100.0)
    fill(T.st[:, 3:128:4], 32, 49.0 / 64)
    fill(T.c1[:, 0:128:16], 8, BIG, a_c1)
    fill(T.l0[:, 0:192:2], 96, 0.0)
    fill(T.fs[:, 0:192:3], 64, 0.0)
    fill(T.fd[:, 1:384:3], 128, 0.0)
    for b in range(4):
        fill(T.t2[:, PL * b:PL * b + Z0], Z0, 0.0)
    v_id = ts(T.ebuf[:, 3:515:4], T.diag[:], 0.0, A.is_equal, None, None, i_e, m_e)
    ms(T.zt[:, 256:512], 0.0)

    def unit(b):
        return qz(blk(T.eq, b), blk(T.ep, b), T.ebuf[:, 3 - b:515 - b], v_id)

    v_e = [unit(0), unit(1)]
    v_pp = tr(T.pp[:, 0:64], T.ppin[:, 0:64], i_pp)
    v_e.append(unit(2))
    v_lb = ts(off[:, 0:8], T.io32[:, 0:8], T.pp[:, 0:1], A.add, None, None, v_pp, i_bl)
    v_e.append(unit(3))
    line = T.pp[:, 64:65]

    t32 = T.tl[:, 0:32]
    a_lk = lin(T.io32[:, 8:16], T.tl[:, 0:8], 1.0, -1.5, i_tl)
    a_ab = act(blk(T.k0, 0, 32), t32, AF.Abs, 1.0 / 64, -7.5 / 64)
    lin(T.st[:, 2:128:4], t32, 1.0 / 64, 48.0 / 64)
    lin(blk(T.k0, 1, 32), t32, -1.0 / 64, -48.0 / 64)
    a_k0 = lin(blk(T.k0, 2, 32), blk(T.k0, 0, 32), 1.0, -55.5 / 64, a_ab)
    a_kj = lin(T.kj[:], T.tl[:, 32:128], 1.0 / 64, -63.0 / 64)
    lin(T.l1[:, 0:192:2], T.tl[:, 32:128], 1.0 / 64, 1.0 / 64)

    v_lu = ts(off[:, 16:24], T.tl[:, 0:16:2], 16.0, A.mult, None, None, i_tl)
    v_bt = ts(T.bt[:], T.blrow[:].indirect(off[:, 0:8]), 1.0 / 64, A.mult, -63.0 / 64, A.add, k_bl, v_lb)
    v_lk = ts(off[:, 8:16], T.io32[:, 8:16], T.pp[:, 32:33], A.mult, 48.0, A.add, a_lk)
    v_ln = tr(T.pp[:, 64:96], T.ppin[:, 64:96], i_ln)
    v_an = tr(T.an[:], T.bt[:], v_bt)
    v_qu = qz(T.uq[:], T.up[:], T.uin[:], k_u)
    k_0, k_1 = T.an[:].indirect(off[:, 8:10]), T.an[:].indirect(off[:, 10:16])
    act(T.d0[:, 1:128:4], k_0, AF.Copy, None, None, v_an, v_lk)
    a_n0 = lin(T.d0[:, 3:128:4], k_0, -1.0, -63.0 / 64)
    a_th = act(T.l1[:, 1:192:2], k_1, AF.Copy, -1.0, None)
    act(T.d0[:, 129:512:4], k_1, AF.Copy, None, None)
    a_n1 = lin(T.d0[:, 131:512:4], T.l1[:, 1:192:2], 1.0, -63.0 / 64, a_th)
    a_pu = act(T.up2[:], T.up[:].indirect(off[:, 16:24]), AF.Copy, None, None, v_qu, v_lu)
    for h in range(2):
        lin(T.fd[:, 192 * h + 2:192 * h + 192:3], T.tl[:, 0:128:2], -1.0 / 64 - 1.0 / SC, 2.0 + 15.0 / SC)
    fill(T.dd[:, 127:128], 1, 0.0)
    fill(T.dd[:, 255:C + K], K + 1, 0.0)
    x = fill(T.c2[:, C:C + K], K, 1.0 / 64)
    fill(T.c2[:, C + 16:C + K:16], 3, -15.0 / 64, x)
    fill(T.c2[:, C:C + 1], 1, 0.0)

    sent = [0]

    def send(t, dst, src, sem, *d):
        rid, pid, _se = topo.addr(peers[t])
        eng = topo.engines(core, peers[t])
        wait("g", *d)
        g.remote_dma(dst, src, T.sem["%s%d" % (sem, t)], T.sem.sent, pid, rid, bits(eng))
        sent[0] += len(eng)

    def landed(t, sem, n=1):
        return ("%s%d" % (sem, t), n * len(topo.engines(peers[t], core)))

    def codes(name, t, h):
        return blk(T["%sq%d" % (name, t)], h), blk(T["%sp%d" % (name, t)], h)

    def quant(t, h, src, *d):
        return qz(*codes("x", t, h), blk(src, h, 512), *d)

    def send_x(t, qx):
        send(t, codes("r", t, 0)[0].bitcast(dt.uint8), codes("x", t, 0)[0].bitcast(dt.uint8), "ax", qx[0])
        send(t, T["rp%d" % t][:], T["xp%d" % t][:], "ax", qx[1])
        send(t, codes("r", t, 1)[0].bitcast(dt.uint8), codes("x", t, 1)[0].bitcast(dt.uint8), "ay")

    def sl(buf, s, a):
        return buf[:, 128 * s + a:128 * s + 128:4]

    def lanes(buf, s):
        return buf[:, 64 * s - 63:64 * s:2]

    def tests(s, *d):
        tt(sl(T.st, s, 0), sl(T.st, s, 2), lanes(T.l1, s), A.is_gt, *d)
        tt(sl(T.st, s, 1), sl(T.st, s, 2), lanes(T.l1, s), A.subtract)
        return tt(sl(T.d0, s, 2), sl(T.st, s, 2), lanes(T.lim, s), A.is_le, v_lim)

    def place(s, *d):
        return scan(blk(T.st, s + 1), blk(T.d0, s), blk(T.st, s), 0.0, A.add, A.max, *d)

    def left(buf, a):
        return buf[:, a:a + 505:8]

    def right(buf, a):
        return buf[:, a + 508:a + 3:-8]

    def products(t, qx, *d):
        s = [mm(bank(7 * h, 128), T.uq2[:], T.up2[:], *codes("x", t, h), qx[h], *d) for h in range(2)]
        return s, [mm(bank(1 + b, C), blk(T.eq, b), blk(T.ep, b), T["xq%d" % t][:], T["xp%d" % t][:], v_e[b]) for b in range(4)]

    def keep_t(p):
        return [act(T.tf[:, C * b:C * b + n], bank(1 + b, n), AF.Copy, None, None, p[b]) for b, n in enumerate((C, C, NV))]

    def gap_min(h, *d):
        return scan(blk(T.mm, h), T.c1[:], bank(7 * h, 128), 0.0, A.add, A.min, *d)

    def gap_less(h, *d):
        return tt(T.dd[:, 128 * h:128 * h + 127], bank(7 * h, 128, 1), T.mm[:, 128 * h:128 * h + 127], A.is_lt, *d)

    def gap_last(*d):
        return scan(T.gs[:], T.c2[:], T.dd[:], 1.0, A.add, A.max, *d)

    def gap_mark(*d):
        return lin(T.cols[:, 6:7], T.gs[:, 255:256], 0.5, 1.0, *d)

    gp = T.cols[:, 6:7]

    tt(sl(T.st, 0, 0), k_0, blk(T.k0, 1, 32), A.is_gt, v_an, v_lk, a_k0)
    tt(sl(T.d0, 0, 2), k_0, blk(T.k0, 2, 32), A.is_le)
    x = tt(sl(T.st, 0, 1), k_0, sl(T.st, 0, 2), A.add)
    y = tt(T.l0[:, 1:192:2], k_1, T.kj[:], A.is_le, a_kj)
    x = place(0, x, a_n0)
    v_qx = [quant(0, 0, T.xin, k_x)]
    v_lim = scan(T.lim[:], T.l0[:], T.l1[:], 0.0, A.mult, A.add, y, a_th)
    x = tests(1, x)
    v_pu = cp(T.uq2[:].bitcast(dt.uint32), T.uq[:].bitcast(dt.uint32).indirect(off[:, 16:24]), v_qu, v_lu)
    x = place(1, x, a_n1)
    v_qx.append(quant(0, 1, T.xin, k_x1))
    send_x(0, v_qx)
    p_s, p_d = products(0, v_qx, v_pu, a_pu)
    lin(T.cols[:, 0:1], line, 16.0 / SC, (Z0 - 64.0) / SC)
    lin(T.cols[:, 1:2], line, 16.0 / SC, (Z0 + 64.0) / SC)
    lin(T.cols[:, 2:3], line, 2.0, 1.0)
    for n, c in ((3, 0.0), (4, 15.0), (5, 16.0)):
        a_cols = lin(T.cols[:, n:n + 1], line, 16.0, Z0 + c)
    for k in range(4):
        fill(T.w8[:, 2 * k + 1:128:8], 16, 96.0 - 32 * k)
    fill(T.up1[:, 0:8:2], 4, 1000.0)
    fill(T.dn1[:, 0:8:2], 4, -1000.0)
    lin(T.up1[:, 1:8:2], T.an[:, 0:128:32], 64.0, 62.0)
    lin(T.dn1[:, 1:8:2], T.an[:, 96::-32], -64.0, -62.0)
    x = tests(2, x)
    z0 = gap_min(0, p_s[0])
    x = place(2, x)
    c2 = ts(T.c2[:, 0:C], T.lidx[:], line, A.is_equal, -1.0 / 32, A.mult, i_lx)
    c2 = act(T.c2[:, 15:256:16], T.c2[:, 0:256:16], AF.Copy, -32.0, None, c2)
    x = tests(3, x)
    z1 = gap_min(1, p_s[1])
    x3 = place(3, x)
    gap_less(0, z0)
    a_vh = lin(T.fd[:, 0:192:3], right(T.st, 131), -64.0 / SC, T.cols[:, 1:2], x3, a_cols)
    a_ve = lin(T.fd[:, 192:384:3], left(T.st, 131), 64.0 / SC, T.cols[:, 0:1])
    a_tf = keep_t(p_d)
    v_ww = tt(T.ww[:], left(T.d0, 2), right(T.d0, 2), A.add, x)
    y = scan(T.pi[:], left(T.st, 131), right(T.st, 131), 4.0, A.min, A.add, x3)
    x = scan(T.sg[:], left(T.st, 130), right(T.st, 130), 4.0, A.min, A.add)
    z = gap_less(1, z1)
    tt(T.fs[:, 2:192:3], T.pi[:], T.ww[:], A.is_le, y, v_ww)
    x = ts(T.fs[:, 1:192:3], T.sg[:], 130.0 / 64, A.is_ge, None, None, x)
    v_gp = gap_last(z, c2)
    v_tab = scan(blk(T.tab, 0, 192), T.fs[:], blk(T.fd, 0, 192), 0.0, A.mult, A.add, x, a_vh)
    v_tae = scan(blk(T.tab, 1, 192), T.fs[:], blk(T.fd, 1, 192), 0.0, A.mult, A.add, a_ve)
    a_gp = gap_mark(v_gp)
    for h in range(2):
        lin(T.j8[:, h:128:2], T.lidx[:, 0:256:4], -1.0, T.cols[:, 4 + h:5 + h])
    a_w8 = lin(T.w8[:, 0:128:2], T.w8[:, 1:128:2], 1.0, T.cols[:, 2:3])
    v_p2 = tr(T.pp[:, 96:128], T.ppin[:, 96:128], i_p2)

    v_qv = None
    for t in range(R):
        last = t == R - 1
        if t > 0:
            a_tf = keep_t(p_d)
            z = [gap_min(h, p_s[h]) for h in range(2)]
            v_gp = gap_last([gap_less(h, z[h]) for h in range(2)][1])
            a_gp = gap_mark(v_gp)
        scan(T.se[:, K:2 * K], T.gs[:, C:C + K], T.tab[:, 2:192:3], 0.0, A.min, A.max, v_gp, v_tab)
        x = scan(T.se[:, 0:K], T.gs[:, C:C + K], T.tab[:, 194:384:3], 0.0, A.min, A.max, v_tae)
        if t == 0:
            cp(off[:, 24:32], T.pp[:, 96:104], v_p2)
        send(t, blk(T.lb, t, 8), blk(T.oe, t, 8), "ac", ts(blk(T.oe, t, 8), T.se[:, 15:128:16], gp, A.subtract, SC, A.mult, x, a_gp))
        a_t2 = {}
        for h, banks in enumerate(((5, 6, 1, 2), (0, 7, 5, 6))):
            free = [v_gp, v_gp, a_t2[0, 0], a_t2[1, 0]] if h else [p_d[0], p_d[0]] + a_tf[:2]
            for b in range(4):
                p = mm(bank(banks[b], 128), blk(T.eq, b), blk(T.ep, b), *codes("r", t, h),
                       landed(t, "ay") if h else landed(t, "ax", 2), free[b])
                a = PL * b + Z0 + 128 * h
                a_t2[b, h] = act(T.t2[:, a:a + 128], bank(banks[b], 128), AF.Copy, 0.5, None, p)
        ts(T.lf[:, 0:8:2], T.se[:, 15:K:16], gp, A.subtract, SC, A.mult)
        x = ts(T.lf[:, 1:8:2], T.se[:, K + 15:2 * K:16], gp, A.subtract, SC, A.mult)
        if t == 0:
            ms(T.ha[:, 0:258:2], 0.0)
        scan(T.bb[:, 0:8], T.up1[:], T.lf[:], 0.0, A.add, A.min, x, a_w8)
        x = scan(T.bb[:, 15:7:-1], T.dn1[:], T.lf[:, 7::-1], 0.0, A.add, A.max)
        if t == 0:
            ms(T.hb[:, 0:258:2], 0.0)
        x = tt(T.nf[:], T.bb[:].indirect(off[:, 24:32]), T.j8[:], A.is_lt, x)
        if last:
            ts(T.ob2[:, 0:8:2], T.bb[:, 8:16:2], T.cols[:, 3:4], A.subtract, -1.0, A.max)
            dma("s", "dout", T.ob[:], T.ob2[:], ts(T.ob2[:, 1:8:2], T.bb[:, 1:8:2], T.cols[:, 3:4], A.subtract, -1.0, A.max))
        v_cs = scan(T.cs[:], T.nf[:], T.w8[:], 128.0, A.mult, A.max, x)

        def win(b):
            return blk(T.t2, b, PL)

        e_list, h_list = T.lb[:, 8 * t:8 * t + 4], T.lb[:, 8 * t + 4:8 * t + 8]
        k_c, k_l = landed(t, "ac"), landed(t, "al")
        a_n = [None] + [act(blk(T.nn, b, K), win(b).indirect(h_list), AF.Copy, None, None, k_c, a_t2[b, 1])
                        for b in range(1, 4)]
        a_n[0] = cp(T.nn[:, 0:K], win(0).indirect(h_list), k_c, a_t2[0, 1])
        send(t, blk(T.ld, t, 16), blk(T.lc, t, 16), "al", cp(blk(T.lc, t, 16), T.cs[:, 127:6:-8], v_cs))
        for b in range(4):
            x = tt(T.zt[:, b:256:4], win(b).indirect(e_list), blk(T.nn, b, K), A.add, a_n[b])
        if t == 1:
            v_qv = qz(T.vq[:], T.vp[:], T.vin[:], k_v)
        v_qz = qz(T.zq[:], T.zp[:], T.zt[:], x)
        hk = {0: 1, 3: 7, 2: 2, 1: 0}
        p_h = {b: mm(bank(hk[b], 128), blk(T.wq, b), blk(T.wp, b), T.zq[:], T.zp[:], k_w, v_qz) for b in hk}

        def h_out(b):
            return (T.ha, T.hb)[b // 2][:, 128 * (b % 2) + 1:128 * (b % 2) + 128:2]

        def h_pick(b, a, z):
            return (T.ha, T.hb)[b // 2][:, 128 * (b % 2):128 * (b % 2) + 129].indirect(
                T.ld[:, 16 * t + a // 16:16 * t + z // 16])

        def new(b, a, z):
            return T.xn[:, 4 * a + b:4 * z:4]

        if t == 0:
            k_v = dma("s", "dv", T.vin[:], T.v[:], p_h[2])
        v_h0 = ts(h_out(0), bank(hk[0], K), 0.03125, A.mult, None, None, p_h[0])
        v_h3 = ts(h_out(3), bank(hk[3], K), 0.03125, A.mult, None, None, p_h[3])
        a_h2 = act(h_out(2), bank(hk[2], K), AF.Copy, 0.03125, None, p_h[2])
        a_h1 = act(h_out(1), bank(hk[1], K), AF.Copy, 0.03125, None, p_h[1])
        a_g3 = act(blk(T.g2, 1, C), h_pick(3, 0, C), AF.Copy, None, None, v_h3, k_l)
        a_g2 = act(T.g2[:, NV:C], h_pick(2, NV, C), AF.Copy, None, None, a_h2)
        tt(new(0, 0, C), h_pick(0, 0, C), blk(T.tf, 0, C), A.add, v_h0, k_l)
        tt(new(1, 0, C), h_pick(1, 0, C), blk(T.tf, 1, C), A.add, a_h1)
        tt(new(3, 0, C), blk(T.g2, 1, C), bank(4, C), A.add, a_g3)
        tt(new(2, 0, NV), h_pick(2, 0, NV), T.tf[:, 2 * C:2 * C + NV], A.add)
        x = [tt(new(2, a, z), T.g2[:, a:z], bank(3, z, a), A.add, a_g2) for a, z in ((NV, 128), (128, C))]
        v_qx = [quant(t + 1, h, T.xn, x[h]) for h in range(2)]
        if not last:
            send_x(t + 1, v_qx)
            p_s, p_d = products(t + 1, v_qx)

    p_y = [mm(bank(7 * h, 128), T.vq[:], T.vp[:], *codes("x", R, h), v_qv, v_qx[h]) for h in range(2)]
    y = [cp(blk(T.ys, h), bank(7 * h, 128), p_y[h]) for h in range(2)]
    for h in range(2):
        dma("s", "dout", blk(T.oc, h, 512), codes("x", R, h)[0].bitcast(dt.uint8), v_qx[h])
    for h in range(2):
        dma("s", "dout", blk(T.y, h), blk(T.ys, h), y[h])
    for k in range(4):
        end = dma("a", "dout", T.osc[4 * k:4 * k + 4, :], T["xp%d" % R][32 * k:32 * k + 4, :], v_qx[1])
    wait("g", ("sent", sent[0]), ("sg", cnt["g"]), ("sp", cnt["p"]), ("sv", cnt["v"]), ("sa", cnt["a"]))
    wait("s", end)
